import numpy as np
import ml_dtypes


def mxq(x, axis, fmt="e4m3"):
    dtype, down = {"e4m3": (ml_dtypes.float8_e4m3fn, 7), "e5m2": (ml_dtypes.float8_e5m2, 14)}[fmt]
    v = np.moveaxis(np.asarray(x, np.float32).astype(ml_dtypes.bfloat16).astype(np.float64), axis, -1)
    blocks = v.reshape(v.shape[:-1] + (-1, 32))
    amax = np.abs(blocks).max(-1, keepdims=True)
    byte = np.maximum(np.where(amax > 0, np.frexp(amax)[1] - 1 + 127, 0) - down, 1)
    scale = np.exp2(byte - 127.0)
    codes = (blocks / scale).astype(np.float32).astype(dtype).astype(np.float64)
    return np.moveaxis((codes * scale).reshape(v.shape), -1, axis)


WIDE = False


def mx_kscale(k):
    if not WIDE:
        return np.ones(k)
    levels = np.array([10, -10, 5, -5, 0])
    if k % 512:
        return np.exp2(np.random.permutation(np.resize(levels, k // 32))).repeat(32)
    a = np.empty((k // 512, 16))
    for p in range(k // 512):
        a[p, :8] = np.random.permutation(np.resize(levels, 8))
        for g in range(8):
            far = levels[np.abs(levels - a[p, g]) >= 10]
            a[p, g + 8] = far[np.random.randint(len(far))]
    return np.exp2(a.ravel()).repeat(32)


def f64(x):
    return np.asarray(x).astype(np.float64)


def striped(idx):
    return np.tile(np.asarray(idx).reshape(-1, 16).T, (8, 1)).astype(np.uint16)


def unstriped(offs):
    return offs[:16].T.reshape(-1).astype(np.int64)


E2M1 = np.array([0.0, 0.5, 1.0, 1.5, 2.0, 3.0, 4.0, 6.0, -0.0, -0.5, -1.0, -1.5, -2.0, -3.0, -4.0, -6.0])


def pack_weight(w, fmt):
    k, n = w.shape
    w = f64(np.asarray(w, np.float32).astype(ml_dtypes.bfloat16)).reshape(k // 32, 32, n)
    amax = np.abs(w).max(1)
    if fmt == "e4m3":
        byte = np.frexp(amax)[1] - 1 + 127 - 7
    else:
        mant, ex = np.frexp(amax / 6.0)
        byte = np.where(mant > 0.5, ex, ex - 1) + 127
    byte = np.clip(np.where(amax > 0, byte, 1), 1, 254)
    scaled = (w * np.exp2(127.0 - byte)[:, None, :]).reshape(k, n).astype(np.float32)
    by_word = np.ascontiguousarray(scaled.reshape(k // 512, 128, 4, n).transpose(0, 1, 3, 2))
    if fmt == "e4m3":
        words = by_word.astype(ml_dtypes.float8_e4m3fn).view(np.uint8)
    else:
        c = by_word.astype(ml_dtypes.float4_e2m1fn).view(np.uint8) & 0xF
        words = (c[..., 0::2] | (c[..., 1::2] << 4)).reshape(k // 512, 128, 2 * n)
    return np.ascontiguousarray(words), np.ascontiguousarray(byte.astype(np.uint8).reshape(k // 512, 16, n))


def unpack_weight(words, scales, fmt):
    g, _, n = scales.shape
    words = np.ascontiguousarray(words).reshape(g, 128, n, -1)
    if fmt == "e4m3":
        vals = words.view(ml_dtypes.float8_e4m3fn).astype(np.float64)
    else:
        nib = np.empty((g, 128, n, 4), np.uint8)
        nib[..., 0::2] = words & 0xF
        nib[..., 1::2] = words >> 4
        vals = E2M1[nib]
    vals = vals * np.repeat(np.exp2(scales.astype(np.float64) - 127.0), 8, axis=1)[..., None]
    return vals.transpose(0, 1, 3, 2).reshape(g * 512, n)


def softplus(v):
    return np.log(1.0 + np.exp(v))


B, N, T, D, NQ = 1, 512, 2048, 512, 256


def setup_inputs():
    n = np.random.standard_normal
    idx = np.random.permutation(T)[:B * N]
    s = mx_kscale(D)[:, None]
    kp = pack_weight(n((D, T)) / s, "e4m3")
    return {
        "qT": (n((B, D, NQ)) * s * (1.00 / np.sqrt(D))).astype(np.float32),
        "k_words": kp[0],
        "k_scales": kp[1],
        "ps": (n((B, NQ, 1)) + 1).astype(np.float32),
        "offs": striped(idx),
    }


def reference(qT, k_words, k_scales, ps, offs):
    idx = unstriped(offs)
    pick = lambda x, which: x[:, which].reshape(x.shape[0], B, -1).transpose(1, 0, 2)
    k = unpack_weight(k_words, k_scales, "e4m3")
    kg = pick(k, idx)
    qq = mxq(f64(qT), 1, "e4m3")
    a = qq.transpose(0, 2, 1) @ kg
    m = np.max(a, axis=-1, keepdims=True)
    e = np.exp(a - m)
    l = np.sum(e, axis=-1, keepdims=True)
    y = e / l * softplus(a - f64(ps))
    return y

@@ -1,0 +1,119 @@
+from contextlib import ExitStack
+
+import concourse.mybir as mybir
+
+D, T, N, NQ = 512, 2048, 512, 256
+FLOPS = 2 * NQ * N * D
+
+F32 = mybir.dt.float32
+BF16 = mybir.dt.bfloat16
+I32 = mybir.dt.int32
+U32 = mybir.dt.uint32
+U16 = mybir.dt.uint16
+U8 = mybir.dt.uint8
+FP8X4 = mybir.dt.float8_e4m3fn_x4
+ALU = mybir.AluOpType
+ACT = mybir.ActivationFunctionType
+AX = mybir.AxisListType
+
+P = 128
+PACK = 4
+TILES = NQ // P
+HALF = N // 2
+LIST_COLS = HALF // 16
+FLOOR = 2.0 ** -60
+
+
+def tile_attend_nrm_hard_topk_kernel(tc, qT, k_words, k_scales, ps, offs, out):
+    nc = tc.nc
+    with ExitStack() as ctx:
+        keep = ctx.enter_context(tc.tile_pool(name="keep", bufs=1))
+        psum = ctx.enter_context(tc.psum_pool(name="psum", bufs=1))
+
+        offsets = keep.tile([P, N // 16], U16, name="offsets")
+        nc.sync.dma_start(offsets[:], offs)
+
+        q_raw = keep.tile([P, PACK, NQ], F32, name="q_raw")
+        nc.scalar.dma_start(q_raw[:], qT[0].rearrange("(p j) q -> p j q", j=PACK))
+        pool_words = keep.tile([P, T], I32, name="pool_words", align_bytes=64)
+        nc.scalar.dma_start(pool_words[:], k_words[0].rearrange("p t r -> p (t r)").bitcast(I32))
+
+        pool_scales = keep.tile([P, T], U8, name="pool_scales", align_bytes=64)
+        nc.vector.memset(pool_scales[:].bitcast(I32), 0)
+        for r in range(4):
+            nc.sync.dma_start(pool_scales[r:P:32, :].bitcast(I32), k_scales[0][r:16:4, :].bitcast(I32))
+        pos = keep.tile([P, TILES], F32, name="pos")
+        nc.sync.dma_start(pos[:], ps[0].rearrange("(p t) o -> p (t o)", t=TILES))
+
+        warm_in = keep.tile([P, 1], F32, name="warm_in")
+        warm_out = keep.tile([P, 1], F32, name="warm_out")
+        nc.vector.memset(warm_in[:], 0.0)
+        nc.scalar.activation(warm_out[:], warm_in[:], ACT.Exp)
+
+        key_scales = keep.tile([P, N], U8, name="key_scales", align_bytes=64)
+        nc.vector.tensor_copy(key_scales[:], pool_scales[:].indirect(offsets[:]))
+
+        q_bf = keep.tile([P, TILES, P, PACK], BF16, name="q_bf", align_bytes=64)
+        q_src = q_raw[:].rearrange("p j (m t) -> p t m j", t=TILES)
+        nc.scalar.copy(q_bf[:], q_src)
+        q_codes = keep.tile([P, NQ], U32, name="q_codes", align_bytes=64)
+        q_scales = keep.tile([P, NQ], U8, name="q_scales", align_bytes=64)
+        nc.vector.quantize_mx(out=q_codes[:].bitcast(FP8X4), scales=q_scales[:], in_=q_bf[:].rearrange("p t m j -> p (t m j)"))
+
+        stats = keep.tile([P, TILES, 3], F32, name="stats")
+        nc.vector.tensor_scalar(stats[:, :, 1], pos[:], -1.0, None, ALU.mult)
+
+        key_words = [keep.tile([P, HALF], U32, name="key_words%d" % h, align_bytes=64) for h in range(2)]
+        for h in range(2):
+            nc.vector.tensor_copy(key_words[h][:], pool_words[:].bitcast(U32).indirect(offsets[:, h * LIST_COLS:(h + 1) * LIST_COLS]))
+
+        parts = [(t, h) for h in range(2) for t in range(TILES)]
+        scores, expo = {}, {}
+        sums = keep.tile([P, TILES, 2], F32, name="sums")
+        for t, h in parts:
+            rows = slice(t * P, (t + 1) * P)
+            scores[t, h] = psum.tile([P, HALF], F32, name="scores%d%d" % (t, h))
+            nc.tensor.matmul_mx(
+                out=scores[t, h][:],
+                lhsT=q_codes[:, rows].bitcast(FP8X4),
+                lhsT_scale=q_scales[:, rows],
+                rhs=key_words[h][:].bitcast(FP8X4),
+                rhs_scale=key_scales[:, h * HALF:(h + 1) * HALF],
+                start=True,
+                stop=True,
+            )
+        for t, h in parts:
+            neg_max = stats[:, t, 2 * h:2 * h + 1]
+            nc.vector.tensor_reduce(neg_max, scores[t, h][:], AX.X, ALU.max, negate=True)
+            expo[t, h] = keep.tile([P, HALF], F32, name="expo%d%d" % (t, h))
+            nc.scalar.activation(expo[t, h][:], scores[t, h][:], ACT.Exp, bias=neg_max, accum_out=sums[:, t, 1 - h:2 - h])
+
+        gaps = keep.tile([P, TILES, 6], F32, name="gaps")
+        for t in range(TILES):
+            nc.vector.tensor_scalar(gaps[:, t, 0:2], stats[:, t, 1:3], stats[:, t, 0:1], 0.0, ALU.subtract, ALU.max)
+            nc.vector.tensor_scalar(gaps[:, t, 2:4], stats[:, t, 0:2], stats[:, t, 2:3], 0.0, ALU.subtract, ALU.max)
+            nc.vector.tensor_scalar(gaps[:, t, 4:6], stats[:, t, 0:3:2], pos[:, t:t + 1], 0.0, ALU.add, ALU.max)
+        decay = keep.tile([P, TILES, 6], F32, name="decay")
+        nc.scalar.activation(decay[:], gaps[:], ACT.Exp, scale=-1.0)
+
+        ln_bias = keep.tile([P, TILES, 2], F32, name="ln_bias")
+        nc.vector.tensor_scalar(ln_bias[:], decay[:, :, 0:6:3], FLOOR, None, ALU.add)
+        weighted = keep.tile([P, TILES, 2], F32, name="weighted")
+        total = keep.tile([P, TILES], F32, name="total")
+        for t in range(TILES):
+            nc.vector.scalar_tensor_tensor(weighted[:, t, :], decay[:, t, 1:3], 1.0, sums[:, t, :], ALU.mult, ALU.mult, accum_out=total[:, t:t + 1])
+        inverse = keep.tile([P, TILES], F32, name="inverse")
+        nc.vector.reciprocal(inverse[:], total[:])
+
+        weight = {}
+        for t, h in parts:
+            weight[t, h] = keep.tile([P, HALF], F32, name="weight%d%d" % (t, h))
+            nc.vector.tensor_scalar(weight[t, h][:], expo[t, h][:], decay[:, t, 2 - h:3 - h], inverse[:, t:t + 1], ALU.mult, ALU.mult)
+
+        out_rows = out[0].rearrange("(p t) n -> p t n", t=TILES)
+        for t, h in parts:
+            logs = keep.tile([P, HALF], F32, name="logs%d%d" % (t, h))
+            nc.scalar.activation(logs[:], expo[t, h][:], ACT.Ln, bias=ln_bias[:, t, h:h + 1], scale=decay[:, t, 4 + h:5 + h])
+            result = keep.tile([P, HALF], F32, name="result%d%d" % (t, h))
+            nc.vector.scalar_tensor_tensor(result[:], logs[:], gaps[:, t, 3 * h:3 * h + 1], weight[t, h][:], ALU.add, ALU.mult)
+            nc.sync.dma_start(out_rows[:, t, h * HALF:(h + 1) * HALF], result[:])

@@ -21,7 +21,7 @@ PACK = 4
 TILES = NQ // P
 HALF = N // 2
 LIST_COLS = HALF // 16
-FLOOR = 2.0 ** -60
+FLOOR_EXPONENT = -40.0
 
 
 def tile_attend_nrm_hard_topk_kernel(tc, qT, k_words, k_scales, ps, offs, out):
@@ -31,23 +31,22 @@ def tile_attend_nrm_hard_topk_kernel(tc, qT, k_words, k_scales, ps, offs, out):
         psum = ctx.enter_context(tc.psum_pool(name="psum", bufs=1))
 
         offsets = keep.tile([P, N // 16], U16, name="offsets")
-        nc.sync.dma_start(offsets[:], offs)
-
         q_raw = keep.tile([P, PACK, NQ], F32, name="q_raw")
-        nc.scalar.dma_start(q_raw[:], qT[0].rearrange("(p j) q -> p j q", j=PACK))
-        pool_words = keep.tile([P, T], I32, name="pool_words", align_bytes=64)
-        nc.scalar.dma_start(pool_words[:], k_words[0].rearrange("p t r -> p (t r)").bitcast(I32))
-
-        pool_scales = keep.tile([P, T], U8, name="pool_scales", align_bytes=64)
-        nc.vector.memset(pool_scales[:].bitcast(I32), 0)
-        for r in range(4):
-            nc.sync.dma_start(pool_scales[r:P:32, :].bitcast(I32), k_scales[0][r:16:4, :].bitcast(I32))
+        nc.sync.dma_start(q_raw[:], qT[0].rearrange("(p j) q -> p j q", j=PACK))
+        nc.sync.dma_start(offsets[:], offs)
         pos = keep.tile([P, TILES], F32, name="pos")
         nc.sync.dma_start(pos[:], ps[0].rearrange("(p t) o -> p (t o)", t=TILES))
 
+        pool_scales = keep.tile([P, T], U8, name="pool_scales", tag="scales_then_codes", align_bytes=64)
+        nc.vector.memset(pool_scales[:].bitcast(I32), 0)
+        for r in range(4):
+            nc.sync.dma_start(pool_scales[r:P:32, :].bitcast(I32), k_scales[0][r:16:4, :].bitcast(I32))
+
         warm_in = keep.tile([P, 1], F32, name="warm_in")
         warm_out = keep.tile([P, 1], F32, name="warm_out")
-        nc.vector.memset(warm_in[:], 0.0)
+        nc.vector.memset(warm_in[:], FLOOR_EXPONENT)
+        pool_words = keep.tile([P, T], I32, name="pool_words", align_bytes=64)
+        nc.sync.dma_start(pool_words[:], k_words[0].rearrange("p t r -> p (t r)").bitcast(I32))
         nc.scalar.activation(warm_out[:], warm_in[:], ACT.Exp)
 
         key_scales = keep.tile([P, N], U8, name="key_scales", align_bytes=64)
@@ -56,7 +55,7 @@ def tile_attend_nrm_hard_topk_kernel(tc, qT, k_words, k_scales, ps, offs, out):
         q_bf = keep.tile([P, TILES, P, PACK], BF16, name="q_bf", align_bytes=64)
         q_src = q_raw[:].rearrange("p j (m t) -> p t m j", t=TILES)
         nc.scalar.copy(q_bf[:], q_src)
-        q_codes = keep.tile([P, NQ], U32, name="q_codes", align_bytes=64)
+        q_codes = keep.tile([P, NQ], U32, name="q_codes", tag="scales_then_codes", align_bytes=64)
         q_scales = keep.tile([P, NQ], U8, name="q_scales", align_bytes=64)
         nc.vector.quantize_mx(out=q_codes[:].bitcast(FP8X4), scales=q_scales[:], in_=q_bf[:].rearrange("p t m j -> p (t m j)"))
 
@@ -97,7 +96,7 @@ def tile_attend_nrm_hard_topk_kernel(tc, qT, k_words, k_scales, ps, offs, out):
         nc.scalar.activation(decay[:], gaps[:], ACT.Exp, scale=-1.0)
 
         ln_bias = keep.tile([P, TILES, 2], F32, name="ln_bias")
-        nc.vector.tensor_scalar(ln_bias[:], decay[:, :, 0:6:3], FLOOR, None, ALU.add)
+        nc.vector.tensor_scalar(ln_bias[:], decay[:, :, 0:6:3], warm_out[:], None, ALU.add)
         weighted = keep.tile([P, TILES, 2], F32, name="weighted")
         total = keep.tile([P, TILES], F32, name="total")
         for t in range(TILES):

@@ -54,10 +54,15 @@ def tile_attend_nrm_hard_topk_kernel(tc, qT, k_words, k_scales, ps, offs, out):
 
         q_bf = keep.tile([P, TILES, P, PACK], BF16, name="q_bf", align_bytes=64)
         q_src = q_raw[:].rearrange("p j (m t) -> p t m j", t=TILES)
-        nc.scalar.copy(q_bf[:], q_src)
-        q_codes = keep.tile([P, NQ], U32, name="q_codes", tag="scales_then_codes", align_bytes=64)
-        q_scales = keep.tile([P, NQ], U8, name="q_scales", align_bytes=64)
-        nc.vector.quantize_mx(out=q_codes[:].bitcast(FP8X4), scales=q_scales[:], in_=q_bf[:].rearrange("p t m j -> p (t m j)"))
+        nc.vector.tensor_copy(q_bf[:, 0], q_src[:, 0])
+        nc.scalar.copy(q_bf[:, 1], q_src[:, 1])
+        q_codes = [
+            keep.tile([P, P], U32, name="q_codes0", align_bytes=64),
+            keep.tile([P, P], U32, name="q_codes1", tag="scales_then_codes", align_bytes=64),
+        ]
+        q_scales = keep.tile([P, TILES, P], U8, name="q_scales", align_bytes=64)
+        for t in range(TILES):
+            nc.vector.quantize_mx(out=q_codes[t][:].bitcast(FP8X4), scales=q_scales[:, t, :], in_=q_bf[:, t].rearrange("p m j -> p (m j)"))
 
         stats = keep.tile([P, TILES, 3], F32, name="stats")
         nc.vector.tensor_scalar(stats[:, :, 1], pos[:], -1.0, None, ALU.mult)
@@ -70,12 +75,11 @@ def tile_attend_nrm_hard_topk_kernel(tc, qT, k_words, k_scales, ps, offs, out):
         scores, expo = {}, {}
         sums = keep.tile([P, TILES, 2], F32, name="sums")
         for t, h in parts:
-            rows = slice(t * P, (t + 1) * P)
             scores[t, h] = psum.tile([P, HALF], F32, name="scores%d%d" % (t, h))
             nc.tensor.matmul_mx(
                 out=scores[t, h][:],
-                lhsT=q_codes[:, rows].bitcast(FP8X4),
-                lhsT_scale=q_scales[:, rows],
+                lhsT=q_codes[t][:].bitcast(FP8X4),
+                lhsT_scale=q_scales[:, t, :],
                 rhs=key_words[h][:].bitcast(FP8X4),
                 rhs_scale=key_scales[:, h * HALF:(h + 1) * HALF],
                 start=True,

@@ -22,6 +22,7 @@ TILES = NQ // P
 HALF = N // 2
 LIST_COLS = HALF // 16
 FLOOR_EXPONENT = -40.0
+ROW0 = P - 16
 
 
 def tile_attend_nrm_hard_topk_kernel(tc, qT, k_words, k_scales, ps, offs, out):
@@ -30,27 +31,29 @@ def tile_attend_nrm_hard_topk_kernel(tc, qT, k_words, k_scales, ps, offs, out):
         keep = ctx.enter_context(tc.tile_pool(name="keep", bufs=1))
         psum = ctx.enter_context(tc.psum_pool(name="psum", bufs=1))
 
+        pool_scales = keep.tile([P, T], U8, name="pool_scales", tag="scales_then_codes", align_bytes=64)
+        nc.sync.dma_start(pool_scales[ROW0:P, :].bitcast(I32), k_scales[0].bitcast(I32))
+        nc.vector.memset(pool_scales[0:ROW0, :].bitcast(I32), 0)
         offsets = keep.tile([P, N // 16], U16, name="offsets")
+        nc.sync.dma_start(offsets[:], offs)
         q_raw = keep.tile([P, PACK, NQ], F32, name="q_raw")
         nc.sync.dma_start(q_raw[:], qT[0].rearrange("(p j) q -> p j q", j=PACK))
-        nc.sync.dma_start(offsets[:], offs)
-        pos = keep.tile([P, TILES], F32, name="pos")
-        nc.sync.dma_start(pos[:], ps[0].rearrange("(p t) o -> p (t o)", t=TILES))
-
-        pool_scales = keep.tile([P, T], U8, name="pool_scales", tag="scales_then_codes", align_bytes=64)
-        nc.vector.memset(pool_scales[:].bitcast(I32), 0)
-        for r in range(4):
-            nc.sync.dma_start(pool_scales[r:P:32, :].bitcast(I32), k_scales[0][r:16:4, :].bitcast(I32))
+        key_scales = keep.tile([P, N], U8, name="key_scales", align_bytes=64)
+        nc.vector.memset(key_scales[:].bitcast(I32), 0)
 
         warm_in = keep.tile([P, 1], F32, name="warm_in")
         warm_out = keep.tile([P, 1], F32, name="warm_out")
         nc.vector.memset(warm_in[:], FLOOR_EXPONENT)
         pool_words = keep.tile([P, T], I32, name="pool_words", align_bytes=64)
         nc.sync.dma_start(pool_words[:], k_words[0].rearrange("p t r -> p (t r)").bitcast(I32))
+        pos = keep.tile([P, TILES], F32, name="pos")
+        nc.sync.dma_start(pos[:], ps[0].rearrange("(p t) o -> p (t o)", t=TILES))
         nc.scalar.activation(warm_out[:], warm_in[:], ACT.Exp)
 
-        key_scales = keep.tile([P, N], U8, name="key_scales", align_bytes=64)
-        nc.vector.tensor_copy(key_scales[:], pool_scales[:].indirect(offsets[:]))
+        picked = keep.tile([P, N], U8, name="picked", align_bytes=64)
+        nc.vector.tensor_copy(picked[:], pool_scales[:].indirect(offsets[:]))
+        for r in range(4):
+            nc.sync.dma_start(key_scales[r:P:32, :].bitcast(I32), picked[ROW0 + r:P:4, :].bitcast(I32))
 
         q_bf = keep.tile([P, TILES, P, PACK], BF16, name="q_bf", align_bytes=64)
         q_src = q_raw[:].rearrange("p j (m t) -> p t m j", t=TILES)

@@ -23,6 +23,9 @@ HALF = N // 2
 LIST_COLS = HALF // 16
 FLOOR_EXPONENT = -40.0
 ROW0 = P - 16
+SLOTS = 4
+PARTS = [(0, 0, 128, 1), (0, 128, 128, 2), (1, 0, 256, 1), (0, 256, 256, 3), (1, 256, 256, 2)]
+USED = [4, 3]
 
 
 def tile_attend_nrm_hard_topk_kernel(tc, qT, k_words, k_scales, ps, offs, out):
@@ -41,14 +44,14 @@ def tile_attend_nrm_hard_topk_kernel(tc, qT, k_words, k_scales, ps, offs, out):
         key_scales = keep.tile([P, N], U8, name="key_scales", align_bytes=64)
         nc.vector.memset(key_scales[:].bitcast(I32), 0)
 
-        warm_in = keep.tile([P, 1], F32, name="warm_in")
-        warm_out = keep.tile([P, 1], F32, name="warm_out")
+        warm_in = keep.tile([P, TILES], F32, name="warm_in")
+        sums = keep.tile([P, TILES, SLOTS], F32, name="sums")
         nc.vector.memset(warm_in[:], FLOOR_EXPONENT)
         pool_words = keep.tile([P, T], I32, name="pool_words", align_bytes=64)
         nc.sync.dma_start(pool_words[:], k_words[0].rearrange("p t r -> p (t r)").bitcast(I32))
         pos = keep.tile([P, TILES], F32, name="pos")
         nc.sync.dma_start(pos[:], ps[0].rearrange("(p t) o -> p (t o)", t=TILES))
-        nc.scalar.activation(warm_out[:], warm_in[:], ACT.Exp)
+        nc.scalar.activation(sums[:, :, 0], warm_in[:], ACT.Exp)
 
         picked = keep.tile([P, N], U8, name="picked", align_bytes=64)
         nc.vector.tensor_copy(picked[:], pool_scales[:].indirect(offsets[:]))
@@ -67,59 +70,61 @@ def tile_attend_nrm_hard_topk_kernel(tc, qT, k_words, k_scales, ps, offs, out):
         for t in range(TILES):
             nc.vector.quantize_mx(out=q_codes[t][:].bitcast(FP8X4), scales=q_scales[:, t, :], in_=q_bf[:, t].rearrange("p m j -> p (m j)"))
 
-        stats = keep.tile([P, TILES, 3], F32, name="stats")
-        nc.vector.tensor_scalar(stats[:, :, 1], pos[:], -1.0, None, ALU.mult)
+        stats = keep.tile([P, TILES, SLOTS], F32, name="stats")
+        nc.vector.tensor_scalar(stats[:, :, 0], pos[:], -1.0, None, ALU.mult)
+        nc.vector.tensor_scalar(stats[:, 1, 3:4], pos[:, 1:2], -1.0, None, ALU.mult)
 
         key_words = [keep.tile([P, HALF], U32, name="key_words%d" % h, align_bytes=64) for h in range(2)]
         for h in range(2):
             nc.vector.tensor_copy(key_words[h][:], pool_words[:].bitcast(U32).indirect(offsets[:, h * LIST_COLS:(h + 1) * LIST_COLS]))
 
-        parts = [(t, h) for h in range(2) for t in range(TILES)]
-        scores, expo = {}, {}
-        sums = keep.tile([P, TILES, 2], F32, name="sums")
-        for t, h in parts:
-            scores[t, h] = psum.tile([P, HALF], F32, name="scores%d%d" % (t, h))
+        scores, expo = [], []
+        for i, (t, c0, w, s) in enumerate(PARTS):
+            scores.append(psum.tile([P, w], F32, name="scores%d" % i))
             nc.tensor.matmul_mx(
-                out=scores[t, h][:],
+                out=scores[i][:],
                 lhsT=q_codes[t][:].bitcast(FP8X4),
                 lhsT_scale=q_scales[:, t, :],
-                rhs=key_words[h][:].bitcast(FP8X4),
-                rhs_scale=key_scales[:, h * HALF:(h + 1) * HALF],
+                rhs=key_words[c0 // HALF][:, c0 % HALF:c0 % HALF + w].bitcast(FP8X4),
+                rhs_scale=key_scales[:, c0:c0 + w],
                 start=True,
                 stop=True,
             )
-        for t, h in parts:
-            neg_max = stats[:, t, 2 * h:2 * h + 1]
-            nc.vector.tensor_reduce(neg_max, scores[t, h][:], AX.X, ALU.max, negate=True)
-            expo[t, h] = keep.tile([P, HALF], F32, name="expo%d%d" % (t, h))
-            nc.scalar.activation(expo[t, h][:], scores[t, h][:], ACT.Exp, bias=neg_max, accum_out=sums[:, t, 1 - h:2 - h])
+        for i, (t, c0, w, s) in enumerate(PARTS):
+            neg_max = stats[:, t, s:s + 1]
+            nc.vector.tensor_reduce(neg_max, scores[i][:], AX.X, ALU.max, negate=True)
+            expo.append(keep.tile([P, w], F32, name="expo%d" % i))
+            nc.scalar.activation(expo[i][:], scores[i][:], ACT.Exp, bias=neg_max, accum_out=sums[:, t, s:s + 1])
 
-        gaps = keep.tile([P, TILES, 6], F32, name="gaps")
+        neg_ref = keep.tile([P, TILES], F32, name="neg_ref")
+        nc.vector.tensor_reduce(neg_ref[:], stats[:], AX.X, ALU.min)
+        decay = keep.tile([P, TILES, SLOTS], F32, name="decay")
         for t in range(TILES):
-            nc.vector.tensor_scalar(gaps[:, t, 0:2], stats[:, t, 1:3], stats[:, t, 0:1], 0.0, ALU.subtract, ALU.max)
-            nc.vector.tensor_scalar(gaps[:, t, 2:4], stats[:, t, 0:2], stats[:, t, 2:3], 0.0, ALU.subtract, ALU.max)
-            nc.vector.tensor_scalar(gaps[:, t, 4:6], stats[:, t, 0:3:2], pos[:, t:t + 1], 0.0, ALU.add, ALU.max)
-        decay = keep.tile([P, TILES, 6], F32, name="decay")
-        nc.scalar.activation(decay[:], gaps[:], ACT.Exp, scale=-1.0)
+            nc.scalar.activation(decay[:, t, :], stats[:, t, :], ACT.Exp, scale=-1.0, bias=neg_ref[:, t:t + 1])
 
-        ln_bias = keep.tile([P, TILES, 2], F32, name="ln_bias")
-        nc.vector.tensor_scalar(ln_bias[:], decay[:, :, 0:6:3], warm_out[:], None, ALU.add)
-        weighted = keep.tile([P, TILES, 2], F32, name="weighted")
+        lift = keep.tile([P, TILES], F32, name="lift")
+        nc.vector.tensor_tensor(lift[:], stats[:, :, 0], neg_ref[:], ALU.subtract)
+        ln_bias = keep.tile([P, TILES], F32, name="ln_bias")
+        nc.vector.tensor_tensor(ln_bias[:], decay[:, :, 0], sums[:, :, 0], ALU.add)
+        weighted = keep.tile([P, TILES, SLOTS], F32, name="weighted")
         total = keep.tile([P, TILES], F32, name="total")
         for t in range(TILES):
-            nc.vector.scalar_tensor_tensor(weighted[:, t, :], decay[:, t, 1:3], 1.0, sums[:, t, :], ALU.mult, ALU.mult, accum_out=total[:, t:t + 1])
+            u = USED[t]
+            nc.vector.scalar_tensor_tensor(weighted[:, t, 0:u], decay[:, t, 0:u], 1.0, sums[:, t, 0:u], ALU.mult, ALU.mult, accum_out=total[:, t:t + 1])
         inverse = keep.tile([P, TILES], F32, name="inverse")
         nc.vector.reciprocal(inverse[:], total[:])
 
-        weight = {}
-        for t, h in parts:
-            weight[t, h] = keep.tile([P, HALF], F32, name="weight%d%d" % (t, h))
-            nc.vector.tensor_scalar(weight[t, h][:], expo[t, h][:], decay[:, t, 2 - h:3 - h], inverse[:, t:t + 1], ALU.mult, ALU.mult)
+        weight = []
+        for i, (t, c0, w, s) in enumerate(PARTS):
+            weight.append(keep.tile([P, w], F32, name="weight%d" % i))
+            nc.vector.tensor_scalar(weight[i][:], expo[i][:], decay[:, t, s:s + 1], inverse[:, t:t + 1], ALU.mult, ALU.mult)
 
         out_rows = out[0].rearrange("(p t) n -> p t n", t=TILES)
-        for t, h in parts:
-            logs = keep.tile([P, HALF], F32, name="logs%d%d" % (t, h))
-            nc.scalar.activation(logs[:], expo[t, h][:], ACT.Ln, bias=ln_bias[:, t, h:h + 1], scale=decay[:, t, 4 + h:5 + h])
-            result = keep.tile([P, HALF], F32, name="result%d%d" % (t, h))
-            nc.vector.scalar_tensor_tensor(result[:], logs[:], gaps[:, t, 3 * h:3 * h + 1], weight[t, h][:], ALU.add, ALU.mult)
-            nc.sync.dma_start(out_rows[:, t, h * HALF:(h + 1) * HALF], result[:])
+        result = {(t, h): keep.tile([P, HALF], F32, name="result%d%d" % (t, h)) for t in range(TILES) for h in range(2)}
+        for i, (t, c0, w, s) in enumerate(PARTS):
+            h = c0 // HALF
+            logs = keep.tile([P, w], F32, name="logs%d" % i)
+            nc.scalar.activation(logs[:], expo[i][:], ACT.Ln, bias=ln_bias[:, t:t + 1], scale=decay[:, t, s:s + 1])
+            nc.vector.scalar_tensor_tensor(result[t, h][:, c0 % HALF:c0 % HALF + w], logs[:], lift[:, t:t + 1], weight[i][:], ALU.add, ALU.mult)
+            if (c0 + w) % HALF == 0:
+                nc.sync.dma_start(out_rows[:, t, h * HALF:(h + 1) * HALF], result[t, h][:])

@@ -24,23 +24,28 @@ LIST_COLS = HALF // 16
 FLOOR_EXPONENT = -40.0
 ROW0 = P - 16
 SLOTS = 4
-PARTS = [(0, 0, 128, 1), (0, 128, 128, 2), (1, 0, 256, 1), (0, 256, 256, 3), (1, 256, 256, 2)]
-USED = [4, 3]
+PARTS = [(0, 0, 256, 1), (0, 256, 256, 2), (1, 0, 256, 1), (1, 256, 128, 2), (1, 384, 128, 3)]
+USED = [3, 4]
+RUN = 4
+Q_PIECES = [(0, 128), (128, 128)]
+Q_BLOCKS = [(0, 128), (128, 128)]
 
 
 def tile_attend_nrm_hard_topk_kernel(tc, qT, k_words, k_scales, ps, offs, out):
     nc = tc.nc
     with ExitStack() as ctx:
         keep = ctx.enter_context(tc.tile_pool(name="keep", bufs=1))
+        shared = ctx.enter_context(tc.tile_pool(name="shared", bufs=1))
         psum = ctx.enter_context(tc.psum_pool(name="psum", bufs=1))
 
-        pool_scales = keep.tile([P, T], U8, name="pool_scales", tag="scales_then_codes", align_bytes=64)
-        nc.sync.dma_start(pool_scales[ROW0:P, :].bitcast(I32), k_scales[0].bitcast(I32))
+        pool_scales = shared.tile([P, T], U8, name="pool_scales", offset=0, align_bytes=64)
+        nc.scalar.dma_start(pool_scales[ROW0:P, :].bitcast(I32), k_scales[0].bitcast(I32))
         nc.vector.memset(pool_scales[0:ROW0, :].bitcast(I32), 0)
         offsets = keep.tile([P, N // 16], U16, name="offsets")
         nc.sync.dma_start(offsets[:], offs)
-        q_raw = keep.tile([P, PACK, NQ], F32, name="q_raw")
-        nc.sync.dma_start(q_raw[:], qT[0].rearrange("(p j) q -> p j q", j=PACK))
+        q_rows = qT[0].rearrange("(p j) q -> p j q", j=PACK)
+        q_raw = [keep.tile([P, PACK, w], F32, name="q_raw%d" % i) for i, (c0, w) in enumerate(Q_PIECES)]
+        nc.sync.dma_start(q_raw[0][:], q_rows[:, :, 0:Q_PIECES[0][1]])
         key_scales = keep.tile([P, N], U8, name="key_scales", align_bytes=64)
         nc.vector.memset(key_scales[:].bitcast(I32), 0)
 
@@ -49,30 +54,34 @@ def tile_attend_nrm_hard_topk_kernel(tc, qT, k_words, k_scales, ps, offs, out):
         nc.vector.memset(warm_in[:], FLOOR_EXPONENT)
         pool_words = keep.tile([P, T], I32, name="pool_words", align_bytes=64)
         nc.sync.dma_start(pool_words[:], k_words[0].rearrange("p t r -> p (t r)").bitcast(I32))
-        pos = keep.tile([P, TILES], F32, name="pos")
-        nc.sync.dma_start(pos[:], ps[0].rearrange("(p t) o -> p (t o)", t=TILES))
+        for i, (c0, w) in list(enumerate(Q_PIECES))[1:]:
+            nc.sync.dma_start(q_raw[i][:], q_rows[:, :, c0:c0 + w])
         nc.scalar.activation(sums[:, :, 0], warm_in[:], ACT.Exp)
 
         picked = keep.tile([P, N], U8, name="picked", align_bytes=64)
         nc.vector.tensor_copy(picked[:], pool_scales[:].indirect(offsets[:]))
         for r in range(4):
-            nc.sync.dma_start(key_scales[r:P:32, :].bitcast(I32), picked[ROW0 + r:P:4, :].bitcast(I32))
+            (nc.sync, nc.scalar)[r % 2].dma_start(key_scales[r:P:32, :].bitcast(I32), picked[ROW0 + r:P:4, :].bitcast(I32))
 
-        q_bf = keep.tile([P, TILES, P, PACK], BF16, name="q_bf", align_bytes=64)
-        q_src = q_raw[:].rearrange("p j (m t) -> p t m j", t=TILES)
-        nc.vector.tensor_copy(q_bf[:, 0], q_src[:, 0])
-        nc.scalar.copy(q_bf[:, 1], q_src[:, 1])
-        q_codes = [
-            keep.tile([P, P], U32, name="q_codes0", align_bytes=64),
-            keep.tile([P, P], U32, name="q_codes1", tag="scales_then_codes", align_bytes=64),
-        ]
-        q_scales = keep.tile([P, TILES, P], U8, name="q_scales", align_bytes=64)
-        for t in range(TILES):
-            nc.vector.quantize_mx(out=q_codes[t][:].bitcast(FP8X4), scales=q_scales[:, t, :], in_=q_bf[:, t].rearrange("p m j -> p (m j)"))
+        pos = shared.tile([P, TILES], F32, name="pos", offset=4 * NQ, align_bytes=64)
+        with nc.allow_non_contiguous_dma(reason="one float32 a row of ps"):
+            nc.sync.dma_start(pos[:], ps[0].rearrange("(t p) o -> p (t o)", t=TILES))
+        q_bf = keep.tile([P, NQ, PACK], BF16, name="q_bf", align_bytes=64)
+        q_codes = shared.tile([P, NQ], U32, name="q_codes", offset=0, align_bytes=64)
+        q_scales = keep.tile([P, NQ], U8, name="q_scales", align_bytes=64)
+        for i, (c0, w) in enumerate(Q_PIECES):
+            dst = q_bf[:, c0:c0 + w, :].rearrange("p (c i) j -> p c j i", i=RUN)
+            src = q_raw[i][:].rearrange("p j (c i) -> p c j i", i=RUN)
+            if i == 0:
+                nc.vector.tensor_copy(dst, src)
+            else:
+                nc.scalar.copy(dst, src)
+        for c0, w in Q_BLOCKS:
+            nc.vector.quantize_mx(out=q_codes[:, c0:c0 + w].bitcast(FP8X4), scales=q_scales[:, c0:c0 + w], in_=q_bf[:, c0:c0 + w, :].rearrange("p m j -> p (m j)"))
 
         stats = keep.tile([P, TILES, SLOTS], F32, name="stats")
         nc.vector.tensor_scalar(stats[:, :, 0], pos[:], -1.0, None, ALU.mult)
-        nc.vector.tensor_scalar(stats[:, 1, 3:4], pos[:, 1:2], -1.0, None, ALU.mult)
+        nc.vector.tensor_scalar(stats[:, 0, 3:4], pos[:, 0:1], -1.0, None, ALU.mult)
 
         key_words = [keep.tile([P, HALF], U32, name="key_words%d" % h, align_bytes=64) for h in range(2)]
         for h in range(2):
@@ -83,8 +92,8 @@ def tile_attend_nrm_hard_topk_kernel(tc, qT, k_words, k_scales, ps, offs, out):
             scores.append(psum.tile([P, w], F32, name="scores%d" % i))
             nc.tensor.matmul_mx(
                 out=scores[i][:],
-                lhsT=q_codes[t][:].bitcast(FP8X4),
-                lhsT_scale=q_scales[:, t, :],
+                lhsT=q_codes[:, t * P:(t + 1) * P].bitcast(FP8X4),
+                lhsT_scale=q_scales[:, t * P:(t + 1) * P],
                 rhs=key_words[c0 // HALF][:, c0 % HALF:c0 % HALF + w].bitcast(FP8X4),
                 rhs_scale=key_scales[:, c0:c0 + w],
                 start=True,
@@ -119,7 +128,7 @@ def tile_attend_nrm_hard_topk_kernel(tc, qT, k_words, k_scales, ps, offs, out):
             weight.append(keep.tile([P, w], F32, name="weight%d" % i))
             nc.vector.tensor_scalar(weight[i][:], expo[i][:], decay[:, t, s:s + 1], inverse[:, t:t + 1], ALU.mult, ALU.mult)
 
-        out_rows = out[0].rearrange("(p t) n -> p t n", t=TILES)
+        out_rows = out[0].rearrange("(t p) n -> p t n", t=TILES)
         result = {(t, h): keep.tile([P, HALF], F32, name="result%d%d" % (t, h)) for t in range(TILES) for h in range(2)}
         for i, (t, c0, w, s) in enumerate(PARTS):
             h = c0 // HALF

@@ -23,11 +23,9 @@ HALF = N // 2
 LIST_COLS = HALF // 16
 FLOOR_EXPONENT = -40.0
 ROW0 = P - 16
-SLOTS = 4
-PARTS = [(0, 0, 256, 1), (0, 256, 256, 2), (1, 0, 256, 1), (1, 256, 128, 2), (1, 384, 128, 3)]
-USED = [3, 4]
-RUN = 4
-Q_PIECES = [(0, 128), (128, 128)]
+SLOTS = 5
+PARTS = [(0, 0, 256, 1), (0, 256, 256, 2), (1, 0, 128, 1), (1, 128, 128, 2), (1, 256, 128, 3), (1, 384, 128, 4)]
+USED = [3, 5]
 Q_BLOCKS = [(0, 128), (128, 128)]
 
 
@@ -44,8 +42,8 @@ def tile_attend_nrm_hard_topk_kernel(tc, qT, k_words, k_scales, ps, offs, out):
         offsets = keep.tile([P, N // 16], U16, name="offsets")
         nc.sync.dma_start(offsets[:], offs)
         q_rows = qT[0].rearrange("(p j) q -> p j q", j=PACK)
-        q_raw = [keep.tile([P, PACK, w], F32, name="q_raw%d" % i) for i, (c0, w) in enumerate(Q_PIECES)]
-        nc.sync.dma_start(q_raw[0][:], q_rows[:, :, 0:Q_PIECES[0][1]])
+        q_early = keep.tile([P, PACK, P], F32, name="q_early")
+        nc.sync.dma_start(q_early[:], q_rows[:, :, 0:P])
         key_scales = keep.tile([P, N], U8, name="key_scales", align_bytes=64)
         nc.vector.memset(key_scales[:].bitcast(I32), 0)
 
@@ -54,8 +52,9 @@ def tile_attend_nrm_hard_topk_kernel(tc, qT, k_words, k_scales, ps, offs, out):
         nc.vector.memset(warm_in[:], FLOOR_EXPONENT)
         pool_words = keep.tile([P, T], I32, name="pool_words", align_bytes=64)
         nc.sync.dma_start(pool_words[:], k_words[0].rearrange("p t r -> p (t r)").bitcast(I32))
-        for i, (c0, w) in list(enumerate(Q_PIECES))[1:]:
-            nc.sync.dma_start(q_raw[i][:], q_rows[:, :, c0:c0 + w])
+        q_late = [keep.tile([P, 2, P], F32, name="q_late%d" % u) for u in range(2)]
+        for u in range(2):
+            nc.sync.dma_start(q_late[u][:], q_rows[:, 2 * u:2 * u + 2, P:NQ])
         nc.scalar.activation(sums[:, :, 0], warm_in[:], ACT.Exp)
 
         picked = keep.tile([P, N], U8, name="picked", align_bytes=64)
@@ -69,19 +68,14 @@ def tile_attend_nrm_hard_topk_kernel(tc, qT, k_words, k_scales, ps, offs, out):
         q_bf = keep.tile([P, NQ, PACK], BF16, name="q_bf", align_bytes=64)
         q_codes = shared.tile([P, NQ], U32, name="q_codes", offset=0, align_bytes=64)
         q_scales = keep.tile([P, NQ], U8, name="q_scales", align_bytes=64)
-        for i, (c0, w) in enumerate(Q_PIECES):
-            dst = q_bf[:, c0:c0 + w, :].rearrange("p (c i) j -> p c j i", i=RUN)
-            src = q_raw[i][:].rearrange("p j (c i) -> p c j i", i=RUN)
-            if i == 0:
-                nc.vector.tensor_copy(dst, src)
-            else:
-                nc.scalar.copy(dst, src)
+        nc.vector.tensor_copy(q_bf[:, 0:P, :], q_early[:].rearrange("p j m -> p m j"))
+        for u in range(2):
+            nc.scalar.copy(q_bf[:, P:NQ, 2 * u:2 * u + 2], q_late[u][:].rearrange("p j m -> p m j"))
         for c0, w in Q_BLOCKS:
             nc.vector.quantize_mx(out=q_codes[:, c0:c0 + w].bitcast(FP8X4), scales=q_scales[:, c0:c0 + w], in_=q_bf[:, c0:c0 + w, :].rearrange("p m j -> p (m j)"))
 
         stats = keep.tile([P, TILES, SLOTS], F32, name="stats")
         nc.vector.tensor_scalar(stats[:, :, 0], pos[:], -1.0, None, ALU.mult)
-        nc.vector.tensor_scalar(stats[:, 0, 3:4], pos[:, 0:1], -1.0, None, ALU.mult)
 
         key_words = [keep.tile([P, HALF], U32, name="key_words%d" % h, align_bytes=64) for h in range(2)]
         for h in range(2):
@@ -106,27 +100,26 @@ def tile_attend_nrm_hard_topk_kernel(tc, qT, k_words, k_scales, ps, offs, out):
             nc.scalar.activation(expo[i][:], scores[i][:], ACT.Exp, bias=neg_max, accum_out=sums[:, t, s:s + 1])
 
         neg_ref = keep.tile([P, TILES], F32, name="neg_ref")
-        nc.vector.tensor_reduce(neg_ref[:], stats[:], AX.X, ALU.min)
         decay = keep.tile([P, TILES, SLOTS], F32, name="decay")
-        for t in range(TILES):
-            nc.scalar.activation(decay[:, t, :], stats[:, t, :], ACT.Exp, scale=-1.0, bias=neg_ref[:, t:t + 1])
-
         lift = keep.tile([P, TILES], F32, name="lift")
-        nc.vector.tensor_tensor(lift[:], stats[:, :, 0], neg_ref[:], ALU.subtract)
         ln_bias = keep.tile([P, TILES], F32, name="ln_bias")
-        nc.vector.tensor_tensor(ln_bias[:], decay[:, :, 0], sums[:, :, 0], ALU.add)
         weighted = keep.tile([P, TILES, SLOTS], F32, name="weighted")
         total = keep.tile([P, TILES], F32, name="total")
+        inverse = keep.tile([P, TILES], F32, name="inverse")
+        weight = [keep.tile([P, w], F32, name="weight%d" % i) for i, (t, c0, w, s) in enumerate(PARTS)]
+        for t in range(TILES):
+            u = USED[t]
+            nc.vector.tensor_reduce(neg_ref[:, t:t + 1], stats[:, t, 0:u], AX.X, ALU.min)
+            nc.scalar.activation(decay[:, t, 0:u], stats[:, t, 0:u], ACT.Exp, scale=-1.0, bias=neg_ref[:, t:t + 1])
         for t in range(TILES):
             u = USED[t]
             nc.vector.scalar_tensor_tensor(weighted[:, t, 0:u], decay[:, t, 0:u], 1.0, sums[:, t, 0:u], ALU.mult, ALU.mult, accum_out=total[:, t:t + 1])
-        inverse = keep.tile([P, TILES], F32, name="inverse")
-        nc.vector.reciprocal(inverse[:], total[:])
-
-        weight = []
-        for i, (t, c0, w, s) in enumerate(PARTS):
-            weight.append(keep.tile([P, w], F32, name="weight%d" % i))
-            nc.vector.tensor_scalar(weight[i][:], expo[i][:], decay[:, t, s:s + 1], inverse[:, t:t + 1], ALU.mult, ALU.mult)
+            nc.vector.reciprocal(inverse[:, t:t + 1], total[:, t:t + 1])
+            for i, (tp, c0, w, s) in enumerate(PARTS):
+                if tp == t:
+                    nc.vector.tensor_scalar(weight[i][:], expo[i][:], decay[:, t, s:s + 1], inverse[:, t:t + 1], ALU.mult, ALU.mult)
+        nc.vector.tensor_tensor(ln_bias[:], decay[:, :, 0], sums[:, :, 0], ALU.add)
+        nc.vector.tensor_tensor(lift[:], stats[:, :, 0], neg_ref[:], ALU.subtract)
 
         out_rows = out[0].rearrange("(t p) n -> p t n", t=TILES)
         result = {(t, h): keep.tile([P, HALF], F32, name="result%d%d" % (t, h)) for t in range(TILES) for h in range(2)}

@@ -24,8 +24,8 @@ LIST_COLS = HALF // 16
 FLOOR_EXPONENT = -40.0
 ROW0 = P - 16
 SLOTS = 5
-PARTS = [(0, 0, 256, 1), (0, 256, 256, 2), (1, 0, 128, 1), (1, 128, 128, 2), (1, 256, 128, 3), (1, 384, 128, 4)]
-USED = [3, 5]
+PARTS = [(t, 128 * s, 128, s + 1) for t in range(TILES) for s in range(4)]
+USED = [5, 5]
 Q_BLOCKS = [(0, 128), (128, 128)]
 
 
@@ -106,7 +106,7 @@ def tile_attend_nrm_hard_topk_kernel(tc, qT, k_words, k_scales, ps, offs, out):
         weighted = keep.tile([P, TILES, SLOTS], F32, name="weighted")
         total = keep.tile([P, TILES], F32, name="total")
         inverse = keep.tile([P, TILES], F32, name="inverse")
-        weight = [keep.tile([P, w], F32, name="weight%d" % i) for i, (t, c0, w, s) in enumerate(PARTS)]
+        weight = keep.tile([P, TILES, N], F32, name="weight")
         for t in range(TILES):
             u = USED[t]
             nc.vector.tensor_reduce(neg_ref[:, t:t + 1], stats[:, t, 0:u], AX.X, ALU.min)
@@ -114,19 +114,18 @@ def tile_attend_nrm_hard_topk_kernel(tc, qT, k_words, k_scales, ps, offs, out):
         for t in range(TILES):
             u = USED[t]
             nc.vector.scalar_tensor_tensor(weighted[:, t, 0:u], decay[:, t, 0:u], 1.0, sums[:, t, 0:u], ALU.mult, ALU.mult, accum_out=total[:, t:t + 1])
-            nc.vector.reciprocal(inverse[:, t:t + 1], total[:, t:t + 1])
-            for i, (tp, c0, w, s) in enumerate(PARTS):
-                if tp == t:
-                    nc.vector.tensor_scalar(weight[i][:], expo[i][:], decay[:, t, s:s + 1], inverse[:, t:t + 1], ALU.mult, ALU.mult)
+        nc.vector.reciprocal(inverse[:], total[:])
         nc.vector.tensor_tensor(ln_bias[:], decay[:, :, 0], sums[:, :, 0], ALU.add)
         nc.vector.tensor_tensor(lift[:], stats[:, :, 0], neg_ref[:], ALU.subtract)
+        for i, (t, c0, w, s) in enumerate(PARTS):
+            nc.vector.tensor_scalar(weight[:, t, c0:c0 + w], expo[i][:], decay[:, t, s:s + 1], inverse[:, t:t + 1], ALU.mult, ALU.mult)
 
         out_rows = out[0].rearrange("(t p) n -> p t n", t=TILES)
-        result = {(t, h): keep.tile([P, HALF], F32, name="result%d%d" % (t, h)) for t in range(TILES) for h in range(2)}
-        for i, (t, c0, w, s) in enumerate(PARTS):
-            h = c0 // HALF
-            logs = keep.tile([P, w], F32, name="logs%d" % i)
-            nc.scalar.activation(logs[:], expo[i][:], ACT.Ln, bias=ln_bias[:, t:t + 1], scale=decay[:, t, s:s + 1])
-            nc.vector.scalar_tensor_tensor(result[t, h][:, c0 % HALF:c0 % HALF + w], logs[:], lift[:, t:t + 1], weight[i][:], ALU.add, ALU.mult)
-            if (c0 + w) % HALF == 0:
-                nc.sync.dma_start(out_rows[:, t, h * HALF:(h + 1) * HALF], result[t, h][:])
+        for t in range(TILES):
+            for h in range(2):
+                cols = slice(h * HALF, (h + 1) * HALF)
+                logs = keep.tile([P, HALF], F32, name="logs%d%d" % (t, h))
+                nc.scalar.activation(logs[:], weight[:, t, cols], ACT.Ln, bias=ln_bias[:, t:t + 1], scale=total[:, t:t + 1])
+                result = keep.tile([P, HALF], F32, name="result%d%d" % (t, h))
+                nc.vector.scalar_tensor_tensor(result[:], logs[:], lift[:, t:t + 1], weight[:, t, cols], ALU.add, ALU.mult)
+                nc.sync.dma_start(out_rows[:, t, cols], result[:])

@@ -60,7 +60,7 @@ def tile_attend_nrm_hard_topk_kernel(tc, qT, k_words, k_scales, ps, offs, out):
         picked = keep.tile([P, N], U8, name="picked", align_bytes=64)
         nc.vector.tensor_copy(picked[:], pool_scales[:].indirect(offsets[:]))
         for r in range(4):
-            (nc.sync, nc.scalar)[r % 2].dma_start(key_scales[r:P:32, :].bitcast(I32), picked[ROW0 + r:P:4, :].bitcast(I32))
+            nc.scalar.dma_start(key_scales[r:P:32, :].bitcast(I32), picked[ROW0 + r:P:4, :].bitcast(I32))
 
         pos = shared.tile([P, TILES], F32, name="pos", offset=4 * NQ, align_bytes=64)
         with nc.allow_non_contiguous_dma(reason="one float32 a row of ps"):

@@ -19,14 +19,12 @@ AX = mybir.AxisListType
 P = 128
 PACK = 4
 TILES = NQ // P
+PART = 128
+PARTS = N // PART
+LIST_COLS = PART // 16
 HALF = N // 2
-LIST_COLS = HALF // 16
 FLOOR_EXPONENT = -40.0
-ROW0 = P - 16
-SLOTS = 5
-PARTS = [(t, 128 * s, 128, s + 1) for t in range(TILES) for s in range(4)]
-USED = [5, 5]
-Q_BLOCKS = [(0, 128), (128, 128)]
+ROW0, ROW_STEP = 32, 4
 
 
 def tile_attend_nrm_hard_topk_kernel(tc, qT, k_words, k_scales, ps, offs, out):
@@ -37,95 +35,85 @@ def tile_attend_nrm_hard_topk_kernel(tc, qT, k_words, k_scales, ps, offs, out):
         psum = ctx.enter_context(tc.psum_pool(name="psum", bufs=1))
 
         pool_scales = shared.tile([P, T], U8, name="pool_scales", offset=0, align_bytes=64)
-        nc.scalar.dma_start(pool_scales[ROW0:P, :].bitcast(I32), k_scales[0].bitcast(I32))
-        nc.vector.memset(pool_scales[0:ROW0, :].bitcast(I32), 0)
+        nc.vector.memset(pool_scales[:].bitcast(I32), 0)
+        nc.scalar.dma_start(pool_scales[ROW0:ROW0 + 16 * ROW_STEP:ROW_STEP, :].bitcast(I32), k_scales[0].bitcast(I32))
         offsets = keep.tile([P, N // 16], U16, name="offsets")
         nc.sync.dma_start(offsets[:], offs)
-        q_rows = qT[0].rearrange("(p j) q -> p j q", j=PACK)
-        q_early = keep.tile([P, PACK, P], F32, name="q_early")
-        nc.sync.dma_start(q_early[:], q_rows[:, :, 0:P])
+        q_raw = keep.tile([P, PACK, NQ], F32, name="q_raw")
+        nc.sync.dma_start(q_raw[:], qT[0].rearrange("(p j) q -> p j q", j=PACK))
+        pool_words = keep.tile([P, T], I32, name="pool_words", align_bytes=64)
+        nc.sync.dma_start(pool_words[:], k_words[0].rearrange("p t r -> p (t r)").bitcast(I32))
         key_scales = keep.tile([P, N], U8, name="key_scales", align_bytes=64)
         nc.vector.memset(key_scales[:].bitcast(I32), 0)
 
-        warm_in = keep.tile([P, TILES], F32, name="warm_in")
-        sums = keep.tile([P, TILES, SLOTS], F32, name="sums")
-        nc.vector.memset(warm_in[:], FLOOR_EXPONENT)
-        pool_words = keep.tile([P, T], I32, name="pool_words", align_bytes=64)
-        nc.sync.dma_start(pool_words[:], k_words[0].rearrange("p t r -> p (t r)").bitcast(I32))
-        q_late = [keep.tile([P, 2, P], F32, name="q_late%d" % u) for u in range(2)]
-        for u in range(2):
-            nc.sync.dma_start(q_late[u][:], q_rows[:, 2 * u:2 * u + 2, P:NQ])
-        nc.scalar.activation(sums[:, :, 0], warm_in[:], ACT.Exp)
+        floor_in = keep.tile([P, TILES], F32, name="floor_in")
+        sums = keep.tile([P, TILES, PARTS + 1], F32, name="sums")
+        gaps = keep.tile([P, TILES, PARTS + 1], F32, name="gaps")
+        nc.vector.memset(floor_in[:], FLOOR_EXPONENT)
+        nc.vector.memset(gaps[:, :, 0], 0.0)
+        nc.scalar.activation(sums[:, :, 0], floor_in[:], ACT.Exp)
 
         picked = keep.tile([P, N], U8, name="picked", align_bytes=64)
         nc.vector.tensor_copy(picked[:], pool_scales[:].indirect(offsets[:]))
         for r in range(4):
-            nc.scalar.dma_start(key_scales[r:P:32, :].bitcast(I32), picked[ROW0 + r:P:4, :].bitcast(I32))
+            queue = nc.scalar if r < 2 else nc.sync
+            queue.dma_start(key_scales[r:P:32, :].bitcast(I32), picked[ROW0 + ROW_STEP * r:ROW0 + 16 * ROW_STEP:4 * ROW_STEP, :].bitcast(I32))
 
-        pos = shared.tile([P, TILES], F32, name="pos", offset=4 * NQ, align_bytes=64)
-        with nc.allow_non_contiguous_dma(reason="one float32 a row of ps"):
-            nc.sync.dma_start(pos[:], ps[0].rearrange("(t p) o -> p (t o)", t=TILES))
-        q_bf = keep.tile([P, NQ, PACK], BF16, name="q_bf", align_bytes=64)
-        q_codes = shared.tile([P, NQ], U32, name="q_codes", offset=0, align_bytes=64)
+        pos = shared.tile([P, TILES], F32, name="pos", offset=0, align_bytes=64)
+        nc.sync.dma_start(pos[:], ps[0].rearrange("(p t) o -> p (t o)", t=TILES))
+        q_bf = shared.tile([P, TILES, P, PACK], BF16, name="q_bf", offset=64, align_bytes=64)
+        q_codes = keep.tile([P, NQ], U32, name="q_codes", align_bytes=64)
         q_scales = keep.tile([P, NQ], U8, name="q_scales", align_bytes=64)
-        nc.vector.tensor_copy(q_bf[:, 0:P, :], q_early[:].rearrange("p j m -> p m j"))
-        for u in range(2):
-            nc.scalar.copy(q_bf[:, P:NQ, 2 * u:2 * u + 2], q_late[u][:].rearrange("p j m -> p m j"))
-        for c0, w in Q_BLOCKS:
-            nc.vector.quantize_mx(out=q_codes[:, c0:c0 + w].bitcast(FP8X4), scales=q_scales[:, c0:c0 + w], in_=q_bf[:, c0:c0 + w, :].rearrange("p m j -> p (m j)"))
+        nc.vector.tensor_copy(q_bf[:], q_raw[:].rearrange("p j (m t) -> p t m j", t=TILES))
+        nc.vector.quantize_mx(out=q_codes[:].bitcast(FP8X4), scales=q_scales[:], in_=q_bf[:].rearrange("p t m j -> p (t m j)"))
 
-        stats = keep.tile([P, TILES, SLOTS], F32, name="stats")
-        nc.vector.tensor_scalar(stats[:, :, 0], pos[:], -1.0, None, ALU.mult)
+        key_words = [shared.tile([P, PART], U32, name="key_words%d" % s, offset=64 + 4 * PART * s, align_bytes=64) for s in range(PARTS)]
+        for s in range(PARTS):
+            nc.vector.tensor_copy(key_words[s][:], pool_words[:].bitcast(U32).indirect(offsets[:, s * LIST_COLS:(s + 1) * LIST_COLS]))
 
-        key_words = [keep.tile([P, HALF], U32, name="key_words%d" % h, align_bytes=64) for h in range(2)]
-        for h in range(2):
-            nc.vector.tensor_copy(key_words[h][:], pool_words[:].bitcast(U32).indirect(offsets[:, h * LIST_COLS:(h + 1) * LIST_COLS]))
-
-        scores, expo = [], []
-        for i, (t, c0, w, s) in enumerate(PARTS):
-            scores.append(psum.tile([P, w], F32, name="scores%d" % i))
+        steps = [(s, t) for s in range(PARTS) for t in range(TILES)]
+        scores, expo = {}, {}
+        for s, t in steps:
+            scores[s, t] = psum.tile([P, PART], F32, name="scores%d%d" % (s, t))
             nc.tensor.matmul_mx(
-                out=scores[i][:],
+                out=scores[s, t][:],
                 lhsT=q_codes[:, t * P:(t + 1) * P].bitcast(FP8X4),
                 lhsT_scale=q_scales[:, t * P:(t + 1) * P],
-                rhs=key_words[c0 // HALF][:, c0 % HALF:c0 % HALF + w].bitcast(FP8X4),
-                rhs_scale=key_scales[:, c0:c0 + w],
+                rhs=key_words[s][:].bitcast(FP8X4),
+                rhs_scale=key_scales[:, s * PART:(s + 1) * PART],
                 start=True,
                 stop=True,
             )
-        for i, (t, c0, w, s) in enumerate(PARTS):
-            neg_max = stats[:, t, s:s + 1]
-            nc.vector.tensor_reduce(neg_max, scores[i][:], AX.X, ALU.max, negate=True)
-            expo.append(keep.tile([P, w], F32, name="expo%d" % i))
-            nc.scalar.activation(expo[i][:], scores[i][:], ACT.Exp, bias=neg_max, accum_out=sums[:, t, s:s + 1])
+        neg_max = keep.tile([P, TILES, PARTS], F32, name="neg_max")
+        for s, t in steps:
+            nc.vector.tensor_reduce(neg_max[:, t, s:s + 1], scores[s, t][:], AX.X, ALU.max, negate=True)
+            expo[s, t] = keep.tile([P, PART], F32, name="expo%d%d" % (s, t))
+            nc.scalar.activation(expo[s, t][:], scores[s, t][:], ACT.Exp, bias=neg_max[:, t, s:s + 1], accum_out=sums[:, t, s + 1:s + 2])
 
-        neg_ref = keep.tile([P, TILES], F32, name="neg_ref")
-        decay = keep.tile([P, TILES, SLOTS], F32, name="decay")
-        lift = keep.tile([P, TILES], F32, name="lift")
+        least = keep.tile([P, TILES], F32, name="least")
+        decay = keep.tile([P, TILES, PARTS + 1], F32, name="decay")
         ln_bias = keep.tile([P, TILES], F32, name="ln_bias")
-        weighted = keep.tile([P, TILES, SLOTS], F32, name="weighted")
+        weighted = keep.tile([P, TILES, PARTS + 1], F32, name="weighted")
         total = keep.tile([P, TILES], F32, name="total")
         inverse = keep.tile([P, TILES], F32, name="inverse")
         weight = keep.tile([P, TILES, N], F32, name="weight")
         for t in range(TILES):
-            u = USED[t]
-            nc.vector.tensor_reduce(neg_ref[:, t:t + 1], stats[:, t, 0:u], AX.X, ALU.min)
-            nc.scalar.activation(decay[:, t, 0:u], stats[:, t, 0:u], ACT.Exp, scale=-1.0, bias=neg_ref[:, t:t + 1])
+            nc.vector.tensor_scalar(gaps[:, t, 1:], neg_max[:, t, :], pos[:, t:t + 1], 0.0, ALU.add, ALU.min, accum_out=least[:, t:t + 1])
+            nc.scalar.activation(decay[:, t, :], gaps[:, t, :], ACT.Exp, scale=-1.0, bias=least[:, t:t + 1])
         for t in range(TILES):
-            u = USED[t]
-            nc.vector.scalar_tensor_tensor(weighted[:, t, 0:u], decay[:, t, 0:u], 1.0, sums[:, t, 0:u], ALU.mult, ALU.mult, accum_out=total[:, t:t + 1])
+            nc.vector.scalar_tensor_tensor(weighted[:, t, :], decay[:, t, :], 1.0, sums[:, t, :], ALU.mult, ALU.mult, accum_out=total[:, t:t + 1])
         nc.vector.reciprocal(inverse[:], total[:])
         nc.vector.tensor_tensor(ln_bias[:], decay[:, :, 0], sums[:, :, 0], ALU.add)
-        nc.vector.tensor_tensor(lift[:], stats[:, :, 0], neg_ref[:], ALU.subtract)
-        for i, (t, c0, w, s) in enumerate(PARTS):
-            nc.vector.tensor_scalar(weight[:, t, c0:c0 + w], expo[i][:], decay[:, t, s:s + 1], inverse[:, t:t + 1], ALU.mult, ALU.mult)
+        for t in range(TILES):
+            for s in range(PARTS):
+                nc.vector.tensor_scalar(weight[:, t, s * PART:(s + 1) * PART], expo[s, t][:], decay[:, t, s + 1:s + 2], inverse[:, t:t + 1], ALU.mult, ALU.mult)
 
-        out_rows = out[0].rearrange("(t p) n -> p t n", t=TILES)
+        out_rows = out[0].rearrange("(p t) n -> p t n", t=TILES)
         for t in range(TILES):
             for h in range(2):
                 cols = slice(h * HALF, (h + 1) * HALF)
                 logs = keep.tile([P, HALF], F32, name="logs%d%d" % (t, h))
                 nc.scalar.activation(logs[:], weight[:, t, cols], ACT.Ln, bias=ln_bias[:, t:t + 1], scale=total[:, t:t + 1])
                 result = keep.tile([P, HALF], F32, name="result%d%d" % (t, h))
-                nc.vector.scalar_tensor_tensor(result[:], logs[:], lift[:, t:t + 1], weight[:, t, cols], ALU.add, ALU.mult)
+                nc.vector.scalar_tensor_tensor(result[:], logs[:], least[:, t:t + 1], weight[:, t, cols], ALU.subtract, ALU.mult)
                 nc.sync.dma_start(out_rows[:, t, cols], result[:])

@@ -24,7 +24,7 @@ PARTS = N // PART
 LIST_COLS = PART // 16
 HALF = N // 2
 FLOOR_EXPONENT = -40.0
-ROW0, ROW_STEP = 32, 4
+ROW0 = P - 16
 
 
 def tile_attend_nrm_hard_topk_kernel(tc, qT, k_words, k_scales, ps, offs, out):
@@ -35,8 +35,8 @@ def tile_attend_nrm_hard_topk_kernel(tc, qT, k_words, k_scales, ps, offs, out):
         psum = ctx.enter_context(tc.psum_pool(name="psum", bufs=1))
 
         pool_scales = shared.tile([P, T], U8, name="pool_scales", offset=0, align_bytes=64)
-        nc.vector.memset(pool_scales[:].bitcast(I32), 0)
-        nc.scalar.dma_start(pool_scales[ROW0:ROW0 + 16 * ROW_STEP:ROW_STEP, :].bitcast(I32), k_scales[0].bitcast(I32))
+        nc.scalar.dma_start(pool_scales[ROW0:P, :].bitcast(I32), k_scales[0].bitcast(I32))
+        nc.vector.memset(pool_scales[0:ROW0, :].bitcast(I32), 0)
         offsets = keep.tile([P, N // 16], U16, name="offsets")
         nc.sync.dma_start(offsets[:], offs)
         q_raw = keep.tile([P, PACK, NQ], F32, name="q_raw")
@@ -57,7 +57,7 @@ def tile_attend_nrm_hard_topk_kernel(tc, qT, k_words, k_scales, ps, offs, out):
         nc.vector.tensor_copy(picked[:], pool_scales[:].indirect(offsets[:]))
         for r in range(4):
             queue = nc.scalar if r < 2 else nc.sync
-            queue.dma_start(key_scales[r:P:32, :].bitcast(I32), picked[ROW0 + ROW_STEP * r:ROW0 + 16 * ROW_STEP:4 * ROW_STEP, :].bitcast(I32))
+            queue.dma_start(key_scales[r:P:32, :].bitcast(I32), picked[ROW0 + r:P:4, :].bitcast(I32))
 
         pos = shared.tile([P, TILES], F32, name="pos", offset=0, align_bytes=64)
         nc.sync.dma_start(pos[:], ps[0].rearrange("(p t) o -> p (t o)", t=TILES))

@@ -46,12 +46,10 @@ def tile_attend_nrm_hard_topk_kernel(tc, qT, k_words, k_scales, ps, offs, out):
         key_scales = keep.tile([P, N], U8, name="key_scales", align_bytes=64)
         nc.vector.memset(key_scales[:].bitcast(I32), 0)
 
-        floor_in = keep.tile([P, TILES], F32, name="floor_in")
-        sums = keep.tile([P, TILES, PARTS + 1], F32, name="sums")
-        gaps = keep.tile([P, TILES, PARTS + 1], F32, name="gaps")
-        nc.vector.memset(floor_in[:], FLOOR_EXPONENT)
-        nc.vector.memset(gaps[:, :, 0], 0.0)
-        nc.scalar.activation(sums[:, :, 0], floor_in[:], ACT.Exp)
+        floor_in = keep.tile([P, TILES, PARTS], F32, name="floor_in")
+        sums = keep.tile([P, TILES, 2, PARTS], F32, name="sums")
+        nc.gpsimd.memset(floor_in[:], FLOOR_EXPONENT)
+        nc.scalar.activation(sums[:, :, 0, :], floor_in[:], ACT.Exp)
 
         picked = keep.tile([P, N], U8, name="picked", align_bytes=64)
         nc.vector.tensor_copy(picked[:], pool_scales[:].indirect(offsets[:]))
@@ -61,13 +59,13 @@ def tile_attend_nrm_hard_topk_kernel(tc, qT, k_words, k_scales, ps, offs, out):
 
         pos = shared.tile([P, TILES], F32, name="pos", offset=0, align_bytes=64)
         nc.sync.dma_start(pos[:], ps[0].rearrange("(p t) o -> p (t o)", t=TILES))
-        q_bf = shared.tile([P, TILES, P, PACK], BF16, name="q_bf", offset=64, align_bytes=64)
+        q_bf = keep.tile([P, TILES, P, PACK], BF16, name="q_bf", align_bytes=64)
         q_codes = keep.tile([P, NQ], U32, name="q_codes", align_bytes=64)
         q_scales = keep.tile([P, NQ], U8, name="q_scales", align_bytes=64)
         nc.vector.tensor_copy(q_bf[:], q_raw[:].rearrange("p j (m t) -> p t m j", t=TILES))
         nc.vector.quantize_mx(out=q_codes[:].bitcast(FP8X4), scales=q_scales[:], in_=q_bf[:].rearrange("p t m j -> p (t m j)"))
 
-        key_words = [shared.tile([P, PART], U32, name="key_words%d" % s, offset=64 + 4 * PART * s, align_bytes=64) for s in range(PARTS)]
+        key_words = [keep.tile([P, PART], U32, name="key_words%d" % s, align_bytes=64) for s in range(PARTS)]
         for s in range(PARTS):
             nc.vector.tensor_copy(key_words[s][:], pool_words[:].bitcast(U32).indirect(offsets[:, s * LIST_COLS:(s + 1) * LIST_COLS]))
 
@@ -84,29 +82,32 @@ def tile_attend_nrm_hard_topk_kernel(tc, qT, k_words, k_scales, ps, offs, out):
                 start=True,
                 stop=True,
             )
-        neg_max = keep.tile([P, TILES, PARTS], F32, name="neg_max")
+        stats = keep.tile([P, TILES, 2, 8], F32, name="stats")
+        nc.gpsimd.tensor_scalar(stats[:, :, 0, 0:PARTS], pos[:].unsqueeze(2).to_broadcast([P, TILES, PARTS]), -1.0, 0.0, ALU.mult, ALU.add)
         for s, t in steps:
-            nc.vector.tensor_reduce(neg_max[:, t, s:s + 1], scores[s, t][:], AX.X, ALU.max, negate=True)
+            nc.vector.tensor_reduce(stats[:, t, 1, s:s + 1], scores[s, t][:], AX.X, ALU.max, negate=True)
             expo[s, t] = keep.tile([P, PART], F32, name="expo%d%d" % (s, t))
-            nc.scalar.activation(expo[s, t][:], scores[s, t][:], ACT.Exp, bias=neg_max[:, t, s:s + 1], accum_out=sums[:, t, s + 1:s + 2])
+            nc.scalar.activation(expo[s, t][:], scores[s, t][:], ACT.Exp, bias=stats[:, t, 1, s:s + 1], accum_out=sums[:, t, 1, s:s + 1])
 
-        least = keep.tile([P, TILES], F32, name="least")
-        decay = keep.tile([P, TILES, PARTS + 1], F32, name="decay")
+        neg_ref = keep.tile([P, TILES], F32, name="neg_ref")
+        lift = keep.tile([P, TILES], F32, name="lift")
+        decay = keep.tile([P, TILES, 2, PARTS], F32, name="decay")
         ln_bias = keep.tile([P, TILES], F32, name="ln_bias")
-        weighted = keep.tile([P, TILES, PARTS + 1], F32, name="weighted")
+        weighted = keep.tile([P, TILES, 2, PARTS], F32, name="weighted")
         total = keep.tile([P, TILES], F32, name="total")
         inverse = keep.tile([P, TILES], F32, name="inverse")
         weight = keep.tile([P, TILES, N], F32, name="weight")
         for t in range(TILES):
-            nc.vector.tensor_scalar(gaps[:, t, 1:], neg_max[:, t, :], pos[:, t:t + 1], 0.0, ALU.add, ALU.min, accum_out=least[:, t:t + 1])
-            nc.scalar.activation(decay[:, t, :], gaps[:, t, :], ACT.Exp, scale=-1.0, bias=least[:, t:t + 1])
+            nc.vector.tensor_reduce(neg_ref[:, t:t + 1], stats[:, t, :, 0:PARTS], AX.XY, ALU.min)
+            nc.scalar.activation(decay[:, t], stats[:, t, :, 0:PARTS], ACT.Exp, scale=-1.0, bias=neg_ref[:, t:t + 1])
         for t in range(TILES):
-            nc.vector.scalar_tensor_tensor(weighted[:, t, :], decay[:, t, :], 1.0, sums[:, t, :], ALU.mult, ALU.mult, accum_out=total[:, t:t + 1])
+            nc.vector.scalar_tensor_tensor(weighted[:, t], decay[:, t], 1.0, sums[:, t], ALU.mult, ALU.mult, accum_out=total[:, t:t + 1])
         nc.vector.reciprocal(inverse[:], total[:])
-        nc.vector.tensor_tensor(ln_bias[:], decay[:, :, 0], sums[:, :, 0], ALU.add)
+        nc.vector.tensor_tensor(ln_bias[:], decay[:, :, 0, 0], sums[:, :, 0, 0], ALU.add)
+        nc.vector.tensor_tensor(lift[:], stats[:, :, 0, 0], neg_ref[:], ALU.subtract)
         for t in range(TILES):
             for s in range(PARTS):
-                nc.vector.tensor_scalar(weight[:, t, s * PART:(s + 1) * PART], expo[s, t][:], decay[:, t, s + 1:s + 2], inverse[:, t:t + 1], ALU.mult, ALU.mult)
+                nc.vector.tensor_scalar(weight[:, t, s * PART:(s + 1) * PART], expo[s, t][:], decay[:, t, 1, s:s + 1], inverse[:, t:t + 1], ALU.mult, ALU.mult)
 
         out_rows = out[0].rearrange("(p t) n -> p t n", t=TILES)
         for t in range(TILES):
@@ -115,5 +116,5 @@ def tile_attend_nrm_hard_topk_kernel(tc, qT, k_words, k_scales, ps, offs, out):
                 logs = keep.tile([P, HALF], F32, name="logs%d%d" % (t, h))
                 nc.scalar.activation(logs[:], weight[:, t, cols], ACT.Ln, bias=ln_bias[:, t:t + 1], scale=total[:, t:t + 1])
                 result = keep.tile([P, HALF], F32, name="result%d%d" % (t, h))
-                nc.vector.scalar_tensor_tensor(result[:], logs[:], least[:, t:t + 1], weight[:, t, cols], ALU.subtract, ALU.mult)
+                nc.vector.scalar_tensor_tensor(result[:], logs[:], lift[:, t:t + 1], weight[:, t, cols], ALU.add, ALU.mult)
                 nc.sync.dma_start(out_rows[:, t, cols], result[:])

@@ -24,7 +24,9 @@ PARTS = N // PART
 LIST_COLS = PART // 16
 HALF = N // 2
 FLOOR_EXPONENT = -40.0
-ROW0 = P - 16
+ROW0 = 32
+ROW_STEP = 4
+ROWS = 16
 
 
 def tile_attend_nrm_hard_topk_kernel(tc, qT, k_words, k_scales, ps, offs, out):
@@ -35,12 +37,14 @@ def tile_attend_nrm_hard_topk_kernel(tc, qT, k_words, k_scales, ps, offs, out):
         psum = ctx.enter_context(tc.psum_pool(name="psum", bufs=1))
 
         pool_scales = shared.tile([P, T], U8, name="pool_scales", offset=0, align_bytes=64)
-        nc.scalar.dma_start(pool_scales[ROW0:P, :].bitcast(I32), k_scales[0].bitcast(I32))
-        nc.vector.memset(pool_scales[0:ROW0, :].bitcast(I32), 0)
+        nc.vector.memset(pool_scales[:].bitcast(I32), 0)
+        q_raw = keep.tile([P, PACK, NQ], F32, name="q_raw")
+        q_rows = qT[0].rearrange("(p j) q -> p j q", j=PACK)
+        nc.sync.dma_start(q_raw[:, 0:2, :], q_rows[:, 0:2, :])
         offsets = keep.tile([P, N // 16], U16, name="offsets")
         nc.sync.dma_start(offsets[:], offs)
-        q_raw = keep.tile([P, PACK, NQ], F32, name="q_raw")
-        nc.sync.dma_start(q_raw[:], qT[0].rearrange("(p j) q -> p j q", j=PACK))
+        nc.sync.dma_start(pool_scales[ROW0:ROW0 + ROWS * ROW_STEP:ROW_STEP, :].bitcast(I32), k_scales[0].bitcast(I32))
+        nc.sync.dma_start(q_raw[:, 2:4, :], q_rows[:, 2:4, :])
         pool_words = keep.tile([P, T], I32, name="pool_words", align_bytes=64)
         nc.sync.dma_start(pool_words[:], k_words[0].rearrange("p t r -> p (t r)").bitcast(I32))
         key_scales = keep.tile([P, N], U8, name="key_scales", align_bytes=64)
@@ -55,7 +59,7 @@ def tile_attend_nrm_hard_topk_kernel(tc, qT, k_words, k_scales, ps, offs, out):
         nc.vector.tensor_copy(picked[:], pool_scales[:].indirect(offsets[:]))
         for r in range(4):
             queue = nc.scalar if r < 2 else nc.sync
-            queue.dma_start(key_scales[r:P:32, :].bitcast(I32), picked[ROW0 + r:P:4, :].bitcast(I32))
+            queue.dma_start(key_scales[r:P:32, :].bitcast(I32), picked[ROW0 + r * ROW_STEP:ROW0 + ROWS * ROW_STEP:4 * ROW_STEP, :].bitcast(I32))
 
         pos = shared.tile([P, TILES], F32, name="pos", offset=0, align_bytes=64)
         nc.sync.dma_start(pos[:], ps[0].rearrange("(p t) o -> p (t o)", t=TILES))

@@ -40,11 +40,11 @@ def tile_attend_nrm_hard_topk_kernel(tc, qT, k_words, k_scales, ps, offs, out):
         nc.vector.memset(pool_scales[:].bitcast(I32), 0)
         q_raw = keep.tile([P, PACK, NQ], F32, name="q_raw")
         q_rows = qT[0].rearrange("(p j) q -> p j q", j=PACK)
-        nc.sync.dma_start(q_raw[:, 0:2, :], q_rows[:, 0:2, :])
+        nc.sync.dma_start(q_raw[0:P:2], q_rows[0:P:2])
         offsets = keep.tile([P, N // 16], U16, name="offsets")
         nc.sync.dma_start(offsets[:], offs)
         nc.sync.dma_start(pool_scales[ROW0:ROW0 + ROWS * ROW_STEP:ROW_STEP, :].bitcast(I32), k_scales[0].bitcast(I32))
-        nc.sync.dma_start(q_raw[:, 2:4, :], q_rows[:, 2:4, :])
+        nc.sync.dma_start(q_raw[1:P:2], q_rows[1:P:2])
         pool_words = keep.tile([P, T], I32, name="pool_words", align_bytes=64)
         nc.sync.dma_start(pool_words[:], k_words[0].rearrange("p t r -> p (t r)").bitcast(I32))
         key_scales = keep.tile([P, N], U8, name="key_scales", align_bytes=64)

@@ -23,6 +23,8 @@ PART = 128
 PARTS = N // PART
 LIST_COLS = PART // 16
 HALF = N // 2
+SPANS = 3
+RUNS = (((0,), (1,), (2, 3)), ((0,), (1, 2), (3,)))
 FLOOR_EXPONENT = -40.0
 ROW0 = 32
 ROW_STEP = 4
@@ -50,8 +52,8 @@ def tile_attend_nrm_hard_topk_kernel(tc, qT, k_words, k_scales, ps, offs, out):
         key_scales = keep.tile([P, N], U8, name="key_scales", align_bytes=64)
         nc.vector.memset(key_scales[:].bitcast(I32), 0)
 
-        floor_in = keep.tile([P, TILES, PARTS], F32, name="floor_in")
-        sums = keep.tile([P, TILES, 2, PARTS], F32, name="sums")
+        floor_in = keep.tile([P, TILES, SPANS], F32, name="floor_in")
+        sums = keep.tile([P, TILES, 2, SPANS], F32, name="sums")
         nc.gpsimd.memset(floor_in[:], FLOOR_EXPONENT)
         nc.scalar.activation(sums[:, :, 0, :], floor_in[:], ACT.Exp)
 
@@ -73,45 +75,48 @@ def tile_attend_nrm_hard_topk_kernel(tc, qT, k_words, k_scales, ps, offs, out):
         for s in range(PARTS):
             nc.vector.tensor_copy(key_words[s][:], pool_words[:].bitcast(U32).indirect(offsets[:, s * LIST_COLS:(s + 1) * LIST_COLS]))
 
-        steps = [(s, t) for s in range(PARTS) for t in range(TILES)]
+        steps = [(0, 0), (0, 1), (1, 0), (1, 1), (2, 0), (2, 1)]
         scores, expo = {}, {}
-        for s, t in steps:
-            scores[s, t] = psum.tile([P, PART], F32, name="scores%d%d" % (s, t))
-            nc.tensor.matmul_mx(
-                out=scores[s, t][:],
-                lhsT=q_codes[:, t * P:(t + 1) * P].bitcast(FP8X4),
-                lhsT_scale=q_scales[:, t * P:(t + 1) * P],
-                rhs=key_words[s][:].bitcast(FP8X4),
-                rhs_scale=key_scales[:, s * PART:(s + 1) * PART],
-                start=True,
-                stop=True,
-            )
+        for u, t in steps:
+            run = RUNS[t][u]
+            scores[u, t] = psum.tile([P, len(run) * PART], F32, name="scores%d%d" % (u, t))
+            for i, s in enumerate(run):
+                nc.tensor.matmul_mx(
+                    out=scores[u, t][:, i * PART:(i + 1) * PART],
+                    lhsT=q_codes[:, t * P:(t + 1) * P].bitcast(FP8X4),
+                    lhsT_scale=q_scales[:, t * P:(t + 1) * P],
+                    rhs=key_words[s][:].bitcast(FP8X4),
+                    rhs_scale=key_scales[:, s * PART:(s + 1) * PART],
+                    start=True,
+                    stop=True,
+                )
         stats = keep.tile([P, TILES, 2, 8], F32, name="stats")
-        nc.gpsimd.tensor_scalar(stats[:, :, 0, 0:PARTS], pos[:].unsqueeze(2).to_broadcast([P, TILES, PARTS]), -1.0, 0.0, ALU.mult, ALU.add)
-        for s, t in steps:
-            nc.vector.tensor_reduce(stats[:, t, 1, s:s + 1], scores[s, t][:], AX.X, ALU.max, negate=True)
-            expo[s, t] = keep.tile([P, PART], F32, name="expo%d%d" % (s, t))
-            nc.scalar.activation(expo[s, t][:], scores[s, t][:], ACT.Exp, bias=stats[:, t, 1, s:s + 1], accum_out=sums[:, t, 1, s:s + 1])
+        nc.gpsimd.tensor_scalar(stats[:, :, 0, 0:SPANS], pos[:].unsqueeze(2).to_broadcast([P, TILES, SPANS]), -1.0, 0.0, ALU.mult, ALU.add)
+        for u, t in steps:
+            nc.vector.tensor_reduce(stats[:, t, 1, u:u + 1], scores[u, t][:], AX.X, ALU.max, negate=True)
+            expo[u, t] = keep.tile([P, len(RUNS[t][u]) * PART], F32, name="expo%d%d" % (u, t))
+            nc.scalar.activation(expo[u, t][:], scores[u, t][:], ACT.Exp, bias=stats[:, t, 1, u:u + 1], accum_out=sums[:, t, 1, u:u + 1])
 
         neg_ref = keep.tile([P, TILES], F32, name="neg_ref")
         lift = keep.tile([P, TILES], F32, name="lift")
-        decay = keep.tile([P, TILES, 2, PARTS], F32, name="decay")
+        decay = keep.tile([P, TILES, 2, SPANS], F32, name="decay")
         ln_bias = keep.tile([P, TILES], F32, name="ln_bias")
-        weighted = keep.tile([P, TILES, 2, PARTS], F32, name="weighted")
+        weighted = keep.tile([P, TILES, 2, SPANS], F32, name="weighted")
         total = keep.tile([P, TILES], F32, name="total")
         inverse = keep.tile([P, TILES], F32, name="inverse")
         weight = keep.tile([P, TILES, N], F32, name="weight")
         for t in range(TILES):
-            nc.vector.tensor_reduce(neg_ref[:, t:t + 1], stats[:, t, :, 0:PARTS], AX.XY, ALU.min)
-            nc.scalar.activation(decay[:, t], stats[:, t, :, 0:PARTS], ACT.Exp, scale=-1.0, bias=neg_ref[:, t:t + 1])
+            nc.vector.tensor_reduce(neg_ref[:, t:t + 1], stats[:, t, :, 0:SPANS], AX.XY, ALU.min)
+            nc.scalar.activation(decay[:, t], stats[:, t, :, 0:SPANS], ACT.Exp, scale=-1.0, bias=neg_ref[:, t:t + 1])
         for t in range(TILES):
             nc.vector.scalar_tensor_tensor(weighted[:, t], decay[:, t], 1.0, sums[:, t], ALU.mult, ALU.mult, accum_out=total[:, t:t + 1])
         nc.vector.reciprocal(inverse[:], total[:])
         nc.vector.tensor_tensor(ln_bias[:], decay[:, :, 0, 0], sums[:, :, 0, 0], ALU.add)
         nc.vector.tensor_tensor(lift[:], stats[:, :, 0, 0], neg_ref[:], ALU.subtract)
         for t in range(TILES):
-            for s in range(PARTS):
-                nc.vector.tensor_scalar(weight[:, t, s * PART:(s + 1) * PART], expo[s, t][:], decay[:, t, 1, s:s + 1], inverse[:, t:t + 1], ALU.mult, ALU.mult)
+            for u, run in enumerate(RUNS[t]):
+                cols = slice(run[0] * PART, (run[-1] + 1) * PART)
+                nc.vector.tensor_scalar(weight[:, t, cols], expo[u, t][:], decay[:, t, 1, u:u + 1], inverse[:, t:t + 1], ALU.mult, ALU.mult)
 
         out_rows = out[0].rearrange("(p t) n -> p t n", t=TILES)
         for t in range(TILES):

@@ -42,11 +42,13 @@ def tile_attend_nrm_hard_topk_kernel(tc, qT, k_words, k_scales, ps, offs, out):
         nc.vector.memset(pool_scales[:].bitcast(I32), 0)
         q_raw = keep.tile([P, PACK, NQ], F32, name="q_raw")
         q_rows = qT[0].rearrange("(p j) q -> p j q", j=PACK)
-        nc.sync.dma_start(q_raw[0:P:2], q_rows[0:P:2])
+        for r in range(2):
+            nc.sync.dma_start(q_raw[r:P:4], q_rows[r:P:4])
         offsets = keep.tile([P, N // 16], U16, name="offsets")
         nc.sync.dma_start(offsets[:], offs)
+        nc.sync.dma_start(q_raw[2:P:4], q_rows[2:P:4])
         nc.sync.dma_start(pool_scales[ROW0:ROW0 + ROWS * ROW_STEP:ROW_STEP, :].bitcast(I32), k_scales[0].bitcast(I32))
-        nc.sync.dma_start(q_raw[1:P:2], q_rows[1:P:2])
+        nc.sync.dma_start(q_raw[3:P:4], q_rows[3:P:4])
         pool_words = keep.tile([P, T], I32, name="pool_words", align_bytes=64)
         nc.sync.dma_start(pool_words[:], k_words[0].rearrange("p t r -> p (t r)").bitcast(I32))
         key_scales = keep.tile([P, N], U8, name="key_scales", align_bytes=64)
@@ -54,7 +56,7 @@ def tile_attend_nrm_hard_topk_kernel(tc, qT, k_words, k_scales, ps, offs, out):
 
         floor_in = keep.tile([P, TILES, SPANS], F32, name="floor_in")
         sums = keep.tile([P, TILES, 2, SPANS], F32, name="sums")
-        nc.gpsimd.memset(floor_in[:], FLOOR_EXPONENT)
+        nc.vector.memset(floor_in[:], FLOOR_EXPONENT)
         nc.scalar.activation(sums[:, :, 0, :], floor_in[:], ACT.Exp)
 
         picked = keep.tile([P, N], U8, name="picked", align_bytes=64)

@@ -70,8 +70,11 @@ def tile_attend_nrm_hard_topk_kernel(tc, qT, k_words, k_scales, ps, offs, out):
         q_bf = keep.tile([P, TILES, P, PACK], BF16, name="q_bf", align_bytes=64)
         q_codes = keep.tile([P, NQ], U32, name="q_codes", align_bytes=64)
         q_scales = keep.tile([P, NQ], U8, name="q_scales", align_bytes=64)
-        nc.vector.tensor_copy(q_bf[:], q_raw[:].rearrange("p j (m t) -> p t m j", t=TILES))
-        nc.vector.quantize_mx(out=q_codes[:].bitcast(FP8X4), scales=q_scales[:], in_=q_bf[:].rearrange("p t m j -> p (t m j)"))
+        q_dealt = q_raw[:].rearrange("p j (m t) -> p t m j", t=TILES)
+        for t in range(TILES):
+            nc.vector.tensor_copy(q_bf[:, t], q_dealt[:, t])
+        for t in range(TILES):
+            nc.vector.quantize_mx(out=q_codes[:, t * P:(t + 1) * P].bitcast(FP8X4), scales=q_scales[:, t * P:(t + 1) * P], in_=q_bf[:, t].rearrange("p m j -> p (m j)"))
 
         key_words = [keep.tile([P, PART], U32, name="key_words%d" % s, align_bytes=64) for s in range(PARTS)]
         for s in range(PARTS):

@@ -40,15 +40,15 @@ def tile_attend_nrm_hard_topk_kernel(tc, qT, k_words, k_scales, ps, offs, out):
 
         pool_scales = shared.tile([P, T], U8, name="pool_scales", offset=0, align_bytes=64)
         nc.vector.memset(pool_scales[:].bitcast(I32), 0)
-        q_raw = keep.tile([P, PACK, NQ], F32, name="q_raw")
+        q_low = keep.tile([P, 2, NQ], F32, name="q_low")
+        q_high = keep.tile([P, 2, NQ], F32, name="q_high")
         q_rows = qT[0].rearrange("(p j) q -> p j q", j=PACK)
-        for r in range(2):
-            nc.sync.dma_start(q_raw[r:P:4], q_rows[r:P:4])
+        nc.sync.dma_start(q_low[:], q_rows[:, 0:2, :])
         offsets = keep.tile([P, N // 16], U16, name="offsets")
         nc.sync.dma_start(offsets[:], offs)
-        nc.sync.dma_start(q_raw[2:P:4], q_rows[2:P:4])
+        nc.sync.dma_start(q_high[0:P:2], q_rows[0:P:2, 2:4, :])
         nc.sync.dma_start(pool_scales[ROW0:ROW0 + ROWS * ROW_STEP:ROW_STEP, :].bitcast(I32), k_scales[0].bitcast(I32))
-        nc.sync.dma_start(q_raw[3:P:4], q_rows[3:P:4])
+        nc.sync.dma_start(q_high[1:P:2], q_rows[1:P:2, 2:4, :])
         pool_words = keep.tile([P, T], I32, name="pool_words", align_bytes=64)
         nc.sync.dma_start(pool_words[:], k_words[0].rearrange("p t r -> p (t r)").bitcast(I32))
         key_scales = keep.tile([P, N], U8, name="key_scales", align_bytes=64)
@@ -70,9 +70,10 @@ def tile_attend_nrm_hard_topk_kernel(tc, qT, k_words, k_scales, ps, offs, out):
         q_bf = keep.tile([P, TILES, P, PACK], BF16, name="q_bf", align_bytes=64)
         q_codes = keep.tile([P, NQ], U32, name="q_codes", align_bytes=64)
         q_scales = keep.tile([P, NQ], U8, name="q_scales", align_bytes=64)
-        q_dealt = q_raw[:].rearrange("p j (m t) -> p t m j", t=TILES)
+        high_dealt = q_high[:].rearrange("p j (m t) -> p t m j", t=TILES)
+        nc.scalar.copy(q_bf[:, :, :, 0:2], q_low[:].rearrange("p j (m t) -> p t m j", t=TILES))
         for t in range(TILES):
-            nc.vector.tensor_copy(q_bf[:, t], q_dealt[:, t])
+            nc.vector.tensor_copy(q_bf[:, t, :, 2:4], high_dealt[:, t])
         for t in range(TILES):
             nc.vector.quantize_mx(out=q_codes[:, t * P:(t + 1) * P].bitcast(FP8X4), scales=q_scales[:, t * P:(t + 1) * P], in_=q_bf[:, t].rearrange("p m j -> p (m j)"))
 

from contextlib import ExitStack

import concourse.mybir as mybir

D, T, N, NQ = 512, 2048, 512, 256
FLOPS = 2 * NQ * N * D

F32 = mybir.dt.float32
BF16 = mybir.dt.bfloat16
I32 = mybir.dt.int32
U32 = mybir.dt.uint32
U16 = mybir.dt.uint16
U8 = mybir.dt.uint8
FP8X4 = mybir.dt.float8_e4m3fn_x4
ALU = mybir.AluOpType
ACT = mybir.ActivationFunctionType
AX = mybir.AxisListType

P = 128
PACK = 4
TILES = NQ // P
PART = 128
PARTS = N // PART
LIST_COLS = PART // 16
HALF = N // 2
SPANS = 3
RUNS = (((0,), (1,), (2, 3)), ((0,), (1, 2), (3,)))
FLOOR_EXPONENT = -40.0
ROW0 = 32
ROW_STEP = 4
ROWS = 16


def tile_attend_nrm_hard_topk_kernel(tc, qT, k_words, k_scales, ps, offs, out):
    nc = tc.nc
    with ExitStack() as ctx:
        keep = ctx.enter_context(tc.tile_pool(name="keep", bufs=1))
        shared = ctx.enter_context(tc.tile_pool(name="shared", bufs=1))
        psum = ctx.enter_context(tc.psum_pool(name="psum", bufs=1))

        pool_scales = shared.tile([P, T], U8, name="pool_scales", offset=0, align_bytes=64)
        nc.vector.memset(pool_scales[:].bitcast(I32), 0)
        q_low = keep.tile([P, 2, NQ], F32, name="q_low")
        q_high = keep.tile([P, 2, NQ], F32, name="q_high")
        q_rows = qT[0].rearrange("(p j) q -> p j q", j=PACK)
        nc.sync.dma_start(q_low[:], q_rows[:, 0:2, :])
        offsets = keep.tile([P, N // 16], U16, name="offsets")
        nc.sync.dma_start(offsets[:], offs)
        nc.sync.dma_start(q_high[0:P:2], q_rows[0:P:2, 2:4, :])
        nc.sync.dma_start(pool_scales[ROW0:ROW0 + ROWS * ROW_STEP:ROW_STEP, :].bitcast(I32), k_scales[0].bitcast(I32))
        nc.sync.dma_start(q_high[1:P:2], q_rows[1:P:2, 2:4, :])
        pool_words = keep.tile([P, T], I32, name="pool_words", align_bytes=64)
        nc.sync.dma_start(pool_words[:], k_words[0].rearrange("p t r -> p (t r)").bitcast(I32))
        key_scales = keep.tile([P, N], U8, name="key_scales", align_bytes=64)
        nc.vector.memset(key_scales[:].bitcast(I32), 0)

        floor_in = keep.tile([P, TILES, SPANS], F32, name="floor_in")
        sums = keep.tile([P, TILES, 2, SPANS], F32, name="sums")
        nc.vector.memset(floor_in[:], FLOOR_EXPONENT)
        nc.scalar.activation(sums[:, :, 0, :], floor_in[:], ACT.Exp)

        picked = keep.tile([P, N], U8, name="picked", align_bytes=64)
        nc.vector.tensor_copy(picked[:], pool_scales[:].indirect(offsets[:]))
        for r in range(4):
            queue = nc.scalar if r < 2 else nc.sync
            queue.dma_start(key_scales[r:P:32, :].bitcast(I32), picked[ROW0 + r * ROW_STEP:ROW0 + ROWS * ROW_STEP:4 * ROW_STEP, :].bitcast(I32))

        pos = shared.tile([P, TILES], F32, name="pos", offset=0, align_bytes=64)
        nc.sync.dma_start(pos[:], ps[0].rearrange("(p t) o -> p (t o)", t=TILES))
        q_bf = keep.tile([P, TILES, P, PACK], BF16, name="q_bf", align_bytes=64)
        q_codes = keep.tile([P, NQ], U32, name="q_codes", align_bytes=64)
        q_scales = keep.tile([P, NQ], U8, name="q_scales", align_bytes=64)
        high_dealt = q_high[:].rearrange("p j (m t) -> p t m j", t=TILES)
        nc.scalar.copy(q_bf[:, :, :, 0:2], q_low[:].rearrange("p j (m t) -> p t m j", t=TILES))
        for t in range(TILES):
            nc.vector.tensor_copy(q_bf[:, t, :, 2:4], high_dealt[:, t])
        for t in range(TILES):
            nc.vector.quantize_mx(out=q_codes[:, t * P:(t + 1) * P].bitcast(FP8X4), scales=q_scales[:, t * P:(t + 1) * P], in_=q_bf[:, t].rearrange("p m j -> p (m j)"))

        key_words = [keep.tile([P, PART], U32, name="key_words%d" % s, align_bytes=64) for s in range(PARTS)]
        for s in range(PARTS):
            nc.vector.tensor_copy(key_words[s][:], pool_words[:].bitcast(U32).indirect(offsets[:, s * LIST_COLS:(s + 1) * LIST_COLS]))

        steps = [(0, 0), (0, 1), (1, 0), (1, 1), (2, 0), (2, 1)]
        scores, expo = {}, {}
        for u, t in steps:
            run = RUNS[t][u]
            scores[u, t] = psum.tile([P, len(run) * PART], F32, name="scores%d%d" % (u, t))
            for i, s in enumerate(run):
                nc.tensor.matmul_mx(
                    out=scores[u, t][:, i * PART:(i + 1) * PART],
                    lhsT=q_codes[:, t * P:(t + 1) * P].bitcast(FP8X4),
                    lhsT_scale=q_scales[:, t * P:(t + 1) * P],
                    rhs=key_words[s][:].bitcast(FP8X4),
                    rhs_scale=key_scales[:, s * PART:(s + 1) * PART],
                    start=True,
                    stop=True,
                )
        stats = keep.tile([P, TILES, 2, 8], F32, name="stats")
        nc.gpsimd.tensor_scalar(stats[:, :, 0, 0:SPANS], pos[:].unsqueeze(2).to_broadcast([P, TILES, SPANS]), -1.0, 0.0, ALU.mult, ALU.add)
        for u, t in steps:
            nc.vector.tensor_reduce(stats[:, t, 1, u:u + 1], scores[u, t][:], AX.X, ALU.max, negate=True)
            expo[u, t] = keep.tile([P, len(RUNS[t][u]) * PART], F32, name="expo%d%d" % (u, t))
            nc.scalar.activation(expo[u, t][:], scores[u, t][:], ACT.Exp, bias=stats[:, t, 1, u:u + 1], accum_out=sums[:, t, 1, u:u + 1])

        neg_ref = keep.tile([P, TILES], F32, name="neg_ref")
        lift = keep.tile([P, TILES], F32, name="lift")
        decay = keep.tile([P, TILES, 2, SPANS], F32, name="decay")
        ln_bias = keep.tile([P, TILES], F32, name="ln_bias")
        weighted = keep.tile([P, TILES, 2, SPANS], F32, name="weighted")
        total = keep.tile([P, TILES], F32, name="total")
        inverse = keep.tile([P, TILES], F32, name="inverse")
        weight = keep.tile([P, TILES, N], F32, name="weight")
        for t in range(TILES):
            nc.vector.tensor_reduce(neg_ref[:, t:t + 1], stats[:, t, :, 0:SPANS], AX.XY, ALU.min)
            nc.scalar.activation(decay[:, t], stats[:, t, :, 0:SPANS], ACT.Exp, scale=-1.0, bias=neg_ref[:, t:t + 1])
        for t in range(TILES):
            nc.vector.scalar_tensor_tensor(weighted[:, t], decay[:, t], 1.0, sums[:, t], ALU.mult, ALU.mult, accum_out=total[:, t:t + 1])
        nc.vector.reciprocal(inverse[:], total[:])
        nc.vector.tensor_tensor(ln_bias[:], decay[:, :, 0, 0], sums[:, :, 0, 0], ALU.add)
        nc.vector.tensor_tensor(lift[:], stats[:, :, 0, 0], neg_ref[:], ALU.subtract)
        for t in range(TILES):
            for u, run in enumerate(RUNS[t]):
                cols = slice(run[0] * PART, (run[-1] + 1) * PART)
                nc.vector.tensor_scalar(weight[:, t, cols], expo[u, t][:], decay[:, t, 1, u:u + 1], inverse[:, t:t + 1], ALU.mult, ALU.mult)

        out_rows = out[0].rearrange("(p t) n -> p t n", t=TILES)
        for t in range(TILES):
            for h in range(2):
                cols = slice(h * HALF, (h + 1) * HALF)
                logs = keep.tile([P, HALF], F32, name="logs%d%d" % (t, h))
                nc.scalar.activation(logs[:], weight[:, t, cols], ACT.Ln, bias=ln_bias[:, t:t + 1], scale=total[:, t:t + 1])
                result = keep.tile([P, HALF], F32, name="result%d%d" % (t, h))
                nc.vector.scalar_tensor_tensor(result[:], logs[:], lift[:, t:t + 1], weight[:, t, cols], ALU.add, ALU.mult)
                nc.sync.dma_start(out_rows[:, t, cols], result[:])
